import numpy as np, ml_dtypes
CORES = [24,25,26,27,28,29,30,31]
N = 8
BF = ml_dtypes.bfloat16
V, M, W, TR, RO, CAP = 320, 160, 4096, 4, 3, 28
def spot(a, b, p, q):
    return ((a * (2 * b + 1) >> 4) + a + p * (2 * b + 613) + q * (2 * a + 37)) & (W - 1)
def look(X, a, b, p, q):
    return np.take_along_axis(X, spot(a, b, p, q).reshape(N, 8, 1, 16 * M), 3).reshape(N, 8, 16, 16, M)
def excess(R, z):
    return np.add.reduce(np.maximum(R - z[:, :, :, None, :], 0), axis=2)
def scan(X, G, B, d, z, t):
    ra = np.arange(N)[:, None, None, None]; ga = np.arange(8)[None, :, None, None]; z = z.astype(np.int32)
    n = np.add.reduce((G >= 0).astype(np.int64), axis=2)
    s = np.where((G >= 0) & ((G & 1) == (t & 1)), n[ra, ga, np.maximum(G, 0)], -1)
    e = np.take_along_axis(G, np.argmax(s, axis=2)[:, :, None, :], 2)[:, :, 0]
    e = np.where(np.max(s, axis=2) >= 0, e, -1)
    v = 2 * np.arange(M) + (t & 1); L = G[..., v]; on = L >= 0; a = np.maximum(L, 0)
    old = d[ra, ga, a]; mine = on & (e[ra, ga, a] == v); dv = d[:, :, v][:, :, None, :]
    new = old; pick = look(X, a, v, old, dv); low = excess(pick, z)
    for j in range(1, TR):
        p = (old + j) & 15; R = look(X, a, v, p, dv); x = excess(R, z); w = mine & (x < low)
        low = np.where(w, x, low); new = np.where(w, p, new); pick = np.where(w[:, :, None], R, pick)
    up = np.max(np.where(on[:, :, None], pick, 0), axis=3)
    o = np.take_along_axis(B, a, 3); both = np.concatenate([d, np.roll(d, -1, axis=0)], axis=2); do = both[ra, ga, o]
    dmg = np.where(on, excess(look(X, o, a, do, new), z) - excess(look(X, o, a, do, old), z), -99999)
    k = np.argmax(dmg, axis=2)[:, :, None, :]
    return n[:, :, v], v, L, a, mine, new, up, np.take_along_axis(dmg, k, 2)[:, :, 0], np.take_along_axis(o, k, 2)[:, :, 0]
def graph(rng, S, share):
    m = np.argsort(rng.random((S, V)), axis=1); i = np.arange(S)[:, None]; mate = np.zeros((S, V), np.int64)
    mate[i, m[:, :M]] = m[:, M:]; mate[i, m[:, M:]] = m[:, :M]
    act = 0.3 + 0.7 * rng.random(V); act[rng.random(V) < 0.04] = 0.0
    r = rng.random((S, V))[i, np.minimum(mate, np.arange(V))]
    return np.where(r < share * act * act[mate], mate, -1)
def tidy(tab):
    tab = np.array(tab, np.int64)
    for k in range(1, len(tab)): tab[k] = np.where(np.any(tab[:k] == tab[k], axis=0), -1, tab[k])
    tab = np.take_along_axis(tab, np.argsort(tab < 0, axis=0, kind="stable"), 0)[:16]
    return np.concatenate([tab, np.full((16 - len(tab), V), -1, np.int64)])
def plain(rng, share):
    return tidy(np.concatenate([np.where(rng.random((1, V)) < 0.15, np.arange(V), -1), graph(rng, 16, share)]))
def blocks(rng, own):
    p = rng.permutation(V).reshape(-1, 16); tab = np.zeros((16, V), np.int64)
    o = np.argsort(rng.random((len(p), 16, 16)), axis=2)
    tab[:, p.reshape(-1)] = p[np.arange(len(p))[:, None, None], o].reshape(-1, 16).T
    return tab if own else tidy(np.where(tab == np.arange(V), -1, tab))
def edges():
    return np.concatenate([np.arange(8), np.arange(V - 8, V)])
def corner(rng):
    c = edges(); tab = c[np.argsort(rng.random((16, V)), axis=0)]
    size = rng.choice(np.array([16, 16, 15, 14, 2, 0]), V); size[c] = rng.choice(np.array([16, 16, 15, 14]), 16)
    tab[:2, size == 2] = np.array([[0], [V - 1]])
    for u in (0, V - 1): tab[:, u] = np.concatenate([[V - 2], rng.permutation(c[c != V - 2])])
    tab[:, V - 2] = np.concatenate([[0], rng.permutation(c[1:15]), [V - 1]]); size[[0, V - 2, V - 1]] = 16
    return np.where(np.arange(16)[:, None] < size, tab, -1)
def lift(rng, rec, z, a, v, dv, o, do):
    def ex(x): return np.add.reduce(np.maximum(rec[:, x] - z.reshape((16,) + (1,) * (x.ndim - 1) + (-1,)), 0), axis=0)
    p = np.arange(16)[:, None]; E = ex(spot(a, v, p, dv))
    new = (p + np.argmin(np.stack([np.roll(E, -j, axis=0) for j in range(TR)]), axis=0)) & 15
    F = ex(spot(o[:, None], a, do[:, None], p))
    D = np.take_along_axis(F, np.broadcast_to(new, F.shape), 1) - F
    s = np.where(D > 0, 1 + rng.random(D.shape) + 2 * (np.arange(len(o))[:, None, None] == 0), 0)
    b = np.argmax(s.reshape(-1, s.shape[-1]), axis=0)
    return b & 15, b >> 4
def parts(rng):
    gl = np.stack([np.stack([plain(rng, float(rng.choice(np.array([0.7, 1.0, 1.5, 2.5])))) for g in range(8)]) for r in range(N)])
    rec = (256 * rng.random((N, 8, 16, W)) * (0.4 + 0.6 * rng.random((N, 8, 1, W)))).astype(np.int64)
    val = rng.integers(0, 16, (N, 8, V)); zl = (256 * rng.random((N, 8, 16, M)) ** 1.5).astype(np.int64)
    th = (rng.choice(np.array([4, 40, 200, 1000]), (N, 8, M)) * rng.random((N, 8, M))).astype(np.int64)
    gs = rng.choice(np.array([0.3, 0.5, 0.8]), (N, 8, 1, 1)); full = rng.integers(0, 8, N); gs[np.arange(N), full] = 1.0; th[np.arange(N), full] = rng.integers(0, 8, (N, M))
    nb = rng.integers(0, V, (N, 8, 16, V)) + V * (rng.random((N, 8, 16, V)) < gs)
    return rec, gl, nb, val, zl, th
def pack(rec, gl, nb, val, zl, th):
    return {"rec": rec.reshape(N, 128, W).astype(np.float32).astype(BF), "gl": np.ascontiguousarray(gl.reshape(N, 128, V)).astype(np.int32), "nb": np.ascontiguousarray(nb.reshape(N, 128, V)).astype(np.int32),
            "val": val.astype(np.int32), "zl": zl.reshape(N, 128, M).astype(np.float32).astype(BF), "th": th.astype(np.int32)}
def largest(rec, gl, nb, val, zl):
    return scan(rec.astype(np.int32), gl, nb, val, zl, 0)[7]
def tune(rng, top, want):
    pos = np.argsort(np.argsort(np.where(top > 0, rng.random(top.shape), 2.0), axis=2), axis=2); sel = (pos < want) & (top > 0); coin = rng.random(top.shape)
    low = np.where(coin < 0.5, top - 1, (rng.random(top.shape) * top).astype(np.int64))
    return np.where(sel, low, np.where(coin < 0.1, 4080, np.maximum(top, 0)))
def setup_inputs(rng):
    return pack(*parts(rng))
def setup_inputs_spread(rng):
    rec, gl, nb, val, zl, th = parts(rng)
    rec = (np.exp2(8 * rng.random((N, 8, 1, W))) * rng.random((N, 8, 16, W))).astype(np.int64)
    zl = (np.exp2(8 * rng.random((N, 8, 1, M))) * rng.random((N, 8, 16, M))).astype(np.int64)
    th = np.minimum((np.exp2(12 * rng.random((N, 8, M)) ** 1.5) - 1).astype(np.int64), 4080)
    nb = (2 * V * rng.random((N, 8, 16, V)) ** 1.5).astype(np.int64); val = (16 * rng.random((N, 8, V)) ** 2).astype(np.int64)
    return pack(rec, gl, nb, val, zl, th)
def setup_inputs_ends(rng):
    rec, gl, nb, val, zl, th = parts(rng)
    rec = 255 * np.where(rng.random((N, 8, 1, W)) < 0.8, rng.integers(0, 2, (N, 8, 1, W)), rng.integers(0, 2, (N, 8, 16, W)))
    val = 15 * rng.integers(0, 2, (N, 8, V)); th = 4080 * (rng.random((N, 8, M)) < 0.4).astype(np.int64)
    zl = 255 * np.where(rng.random((N, 8, 1, M)) < 0.6, rng.random((N, 8, 1, M)) < 0.35, rng.random((N, 8, 16, M)) < 0.35).astype(np.int64)
    e = rng.random((N, 8, 16, V)); nb = np.where(e < 0.4, 0, np.where(e < 0.85, 2 * V - 1, nb))
    for r in range(N):
        few = [6, 7] + [int(g) for g in rng.permutation(6)[:2]]
        for g in range(8):
            gl[r, g] = corner(rng) if g in few else tidy(np.concatenate([graph(rng, 14, 1.5), np.zeros((1, V), np.int64), np.full((1, V), V - 1, np.int64)]))
    for g in (6, 7):
        val[:, g, 0] = 15; val[:, g, V - 2] = 0; val[:, g, V - 1] = 0; zl[:, g, :, M - 1] = 0
        th[:, g, M - 1] = np.where(np.arange(N) % 2 == 1, 0, 4080)
        nb[:, g, 15, V - 1] = 2 * V - 1; nb[:, g, 0, 0] = 0 if g == 7 else 2 * V - 1
        hi = [spot(0, V - 2, 15, 0), spot(V - 1, V - 2, 0, 0), spot(2 * V - 1, V - 1, 0, 1), spot(0, 0, 15, 0) if g == 7 else spot(2 * V - 1, 0, 0, 15)]
        lo = [spot(0, V - 2, 0, 0), spot(V - 1, V - 2, 1, 0), spot(2 * V - 1, V - 1, 0, 0), spot(0, 0, 15, 15) if g == 7 else spot(2 * V - 1, 0, 0, 0)]
        for x in lo: rec[:, g, :, x] = 0
        for x in hi: rec[:, g, :, x] = 255
    return pack(rec, gl, nb, val, zl, th)
def setup_inputs_corners(rng):
    rec, gl, nb, val, zl, th = parts(rng); c = edges(); late = []
    for r in range(N):
        for g, k in enumerate(rng.permutation(8)):
            if k == 0:
                ev = np.concatenate([[V - 2], 2 * rng.permutation(M - 1)]); od = 2 * rng.permutation(M) + 1; h = M // 2
                tab = np.full((16, V), -1, np.int64)
                tab[0, ev[:h]] = od[:h]; tab[0, od[:h]] = ev[:h]; tab[0, od[h:]] = ev[:h]; tab[1, od[h:]] = ev[h:]; tab[0, ev[h:]] = od[h:]
                late.append((r, g, ev[:h], od[:h], od[h:]))
            elif k == 1: tab = blocks(rng, True)
            elif k == 2: tab = blocks(rng, False)
            elif k == 3:
                tab = graph(rng, 16, 2.0); tab = tidy(np.where((tab & 1 == 1) & (np.arange(V) & 1 == 1), tab, -1))
            elif k == 4:
                tab = graph(rng, 16, 2.0); off = rng.random(V) < 0.5; tab = tidy(np.where(off | off[tab], -1, tab))
            elif k == 5:
                tab = np.argsort(rng.random((V, V)), axis=1)[:, :16].T; tab = np.where(np.arange(16)[:, None] < rng.integers(0, 17, V), tab, -1)
            elif k == 6:
                tab = c[np.argsort(rng.random((16, V)), axis=0)]; tab[:, c] = np.argsort(rng.random((16, V)), axis=1)[:, :16].T
            else: tab = plain(rng, 1.5)
            gl[r, g] = tab
    m = np.arange(V); e = rng.integers(0, 10, (N, 8, 16, V))
    for k, x in enumerate((0, V - 1, V, 2 * V - 1, m, m + V)): nb = np.where(e == k, x, nb)
    e = rng.integers(0, 4, (N, 8, V)); val = np.where(e == 0, 0, np.where(e == 1, 15, val))
    e = rng.integers(0, 6, (N, 8, 1, M)); zl = np.where(e == 0, 0, np.where(e == 1, 255, zl >> 1))
    want = rng.choice(np.array([0, 1, CAP - 1, CAP, CAP + 1, M]), (N, 8, 1))
    for r, g, v, a, o in late:
        zl[r, g, :, M - 1] = 0; dv = val[r, g, v]; do = val[r, g, o]; q = (np.arange(16) + 1) & 15
        x = spot(a[0], v[0], np.arange(16), dv[0]); y = spot(o[0], a[0], do[0], np.arange(16))
        s = int(np.argmax((x != y) & (x[q] != y[q]))); u = int(q[s])
        rec[r, g, :, int(x[s])] = 255; rec[r, g, :, int(y[u])] = 255; rec[r, g, :, int(x[u])] = 0; rec[r, g, :, int(y[s])] = 0
        p = lift(rng, rec[r, g], zl[r, g][:, v >> 1], a, v, dv, o[None], do[None])[0]
        val[r, g, a] = p; val[r, g, a[0]] = s; nb[r, g][:, a] = o; want[r, g, 0] = M
    th = tune(rng, largest(rec, gl, nb, val, zl), want)
    for r, g, v, a, o in late: th[r, g, M - 1] = 4079
    return pack(rec, gl, nb, val, zl, th)
def setup_inputs_crowd(rng):
    rec, gl, nb, val, zl, th = parts(rng); zl = zl >> 1; ev = 2 * np.arange(M)
    spots = np.array([V, 2 * V - 1, V + M]); cnt = np.array([CAP, CAP + 1, CAP - 1, M, CAP + 1]); want = np.zeros((N, 8, 1), np.int64)
    for r in range(N):
        most = ((2, 3), (4, 5), (3, 2), (5, 4))[r % 4]
        left = [g for g in range(1, 8) if g not in most]
        want[r, left, 0] = cnt if r == 0 else rng.permutation(cnt)
        want[r, most[0], 0] = M; want[r, most[1], 0] = M - 1
        for g in range(8):
            gl[r, g] = plain(rng, 1.5); s = int(rng.choice(spots))
            if g in most:
                od = 2 * rng.permutation(M) + 1; tab = np.full((16, V), -1, np.int64); tab[0, ev] = od; tab[0, od] = ev; gl[r, g] = tab
                o = np.tile(rng.permutation(spots)[:, None], (1, M))
                p, k = lift(rng, rec[r, g], zl[r, g], od, ev, val[r, g, ev], o, val[(r + 1) % N, g][o - V])
                val[r, g, od] = p; nb[r, g] = o[0, 0]; nb[r, g][:, od] = o[k, np.arange(M)]
            elif g == 0: nb[r, g] = (0, V - 1)[r % 2]
            elif g < 5: nb[r, g] = s
            elif g == 5: nb[r, g] = rng.choice(spots, (16, V))
            else: nb[r, g] = np.where(rng.random((16, V)) * CAP < 1, 2 * V - 1 if s == V else V, s)
    top = largest(rec, gl, nb, val, zl); got = np.minimum(np.add.reduce((top > 0).astype(np.int64), axis=2), want[:, :, 0])
    for r in range(N): want[r, 0, 0] = ((31, 0)[r % 2] - int(np.add.reduce(got[r, 1:]))) & 31
    return pack(rec, gl, nb, val, zl, tune(rng, top, want))
def check_inputs(d):
    bad = []
    for k, lo, hi in (("rec", 0, 255), ("gl", -1, V - 1), ("nb", 0, 2 * V - 1), ("val", 0, 15), ("zl", 0, 255), ("th", 0, 4080)):
        x = np.asarray(d[k]).astype(np.float64)
        if not (np.min(x) >= lo and np.max(x) <= hi): bad.append("range of " + k)
        if np.any(x != np.floor(x)): bad.append("whole numbers in " + k)
    g = np.asarray(d["gl"]).reshape(N, 8, 16, V); on = g >= 0; s = np.sort(g, axis=2)
    if np.any(on[:, :, 1:] & ~on[:, :, :-1]): bad.append("gl: a name after an empty slot")
    if np.any((s[:, :, 1:] == s[:, :, :-1]) & (s[:, :, 1:] >= 0)): bad.append("gl: a name twice in one list")
    return bad
def reference(rec, gl, nb, val, zl, th):
    X = rec.astype(np.float32).astype(np.int32).reshape(N, 8, 16, W); G = gl.astype(np.int64).reshape(N, 8, 16, V); B = nb.astype(np.int64).reshape(N, 8, 16, V)
    d = val.astype(np.int64); z = zl.astype(np.float32).astype(np.int32).reshape(N, 8, 16, M); h = th.astype(np.int64); c = np.zeros((N, 1, 1), np.int64)
    for t in range(RO):
        n, v, L, a, mine, new, up, top, who = scan(X, G, B, d, z, t)
        hurt = top > h + (c & 31)
        c = np.add.reduce(hurt.astype(np.int64).reshape(N, 8 * M), axis=1).reshape(N, 1, 1)
        z = np.roll((z + up) >> 1, 1 + t, axis=0)
        w = np.nonzero(mine); d = d + 0; d[w[0], w[1], a[w]] = new[w]
        gh = (hurt & (who >= V)).astype(np.int64); told = (gh == 1) & (np.add.accumulate(gh, axis=2) - gh < CAP)
        w = np.nonzero(told); np.add.at(d, ((w[0] + 1) % N, w[1], who[w] - V), 1); d = d & 15
        w = np.nonzero(hurt & (who < V) & (n < 16) & ~np.any(L == who[:, :, None, :], axis=2))
        G[w[0], w[1], n[w], v[w[2]]] = who[w]
    return {"yl": G.reshape(N, 128, V).astype(np.float32), "yd": d.astype(np.float32), "yz": z.reshape(N, 128, M).astype(np.float32).astype(BF)}

@@ -1,0 +1,726 @@
+from concourse.mybir import AluOpType as A, AxisListType, ActivationFunctionType as F
+
+N, RO, CAP = 8, 3, 28
+BIG = 524288.0
+
+SCRATCH = {}
+VIEW = {}
+_TYPES = {"f": "float32", "i": "int32", "b": "bfloat16", "u": "uint16"}
+_fill = {}
+
+
+def _own(name, width, kind):
+    SCRATCH[name] = ("sbuf", [128, width], _TYPES[kind])
+    VIEW[name] = (name, 0, width)
+
+
+def _put(name, width, kind):
+    tag = "ar" + kind
+    o = _fill.get(tag, 0)
+    VIEW[name] = (tag, o, width)
+    _fill[tag] = o + (width + 15) // 16 * 16
+    SCRATCH[tag] = ("sbuf", [128, _fill[tag]], _TYPES[kind])
+
+
+for _n, _w in (("BLP", 128), ("CM1", 128), ("B1", 128), ("BLC", 128), ("ALL1", 128), ("MIN1", 128), ("NTRI", 128), ("EVW", 128), ("ODW", 128), ("ID", 128),
+               ("VAL", 320), ("NT", 320), ("NH", 320), ("R8", 640), ("SEL8", 128), ("THL", 320), ("SEL0", 128), ("K15", 160), ("K10", 160)):
+    _put(_n, _w, "b")
+for _n, _w in (("ONF", 128), ("LN", 1), ("LN2", 1), ("LK1", 1), ("LC0", 1), ("LC1", 1), ("AC", 20), ("DMP", 20), ("A21", 20), ("CM40", 40),
+               ("MA1", 320), ("M1V", 320), ("V21", 320), ("KC", 160), ("FL", 160), ("IOT", 208),
+               ("AO", 320), ("M2A", 320), ("BU", 320), ("INV", 320), ("CT", 320), ("CK", 640), ("NS", 320), ("KB", 40),
+               ("NG", 320), ("NPF", 320), ("NCF", 320), ("V8F", 160), ("TH2", 20), ("th64", 10), ("YL", 320), ("EMP", 320)):
+    _put(_n, _w, "f")
+for _n, _w in (("LI", 1), ("TI", 20), ("TJ", 20), ("CJ", 14), ("NA", 320), ("PB", 320), ("HA", 320), ("BUI", 320), ("NP", 320), ("NQ", 320), ("YDI", 320), ("YDJ", 320)):
+    _put(_n, _w, "i")
+for _n, _w in (("AOU", 320), ("COFF", 14)):
+    _put(_n, _w, "u")
+LOCAL = set()
+for _k, _l in (("f", (("T1", 320), ("KL", 320), ("R1", 160), ("R2", 80), ("R3", 40), ("R4", 20), ("A3", 60), ("X1", 20), ("X3", 20), ("X4", 20), ("X5", 20),
+                      ("X6", 20), ("X7", 20), ("OF", 20), ("NM", 20), ("DN", 20), ("PX", 40), ("MM2", 40), ("BB2", 40), ("JC", 80), ("J2", 80), ("TP", 100),
+                      ("U", 40), ("B40", 40), ("PQ", 40), ("UC", 160), ("S1", 160), ("QE", 160), ("QY", 160), ("S2", 160), ("HF", 16),
+                      ("CC", 2), ("JA", 160), ("J3", 30),
+                      ("thr", 10), ("gh", 10), ("xh", 10), ("cs", 10), ("pre", 10), ("prf", 10), ("w", 10), ("cd", 10), ("pu", 10), ("oo", 10), ("op", 10),
+                      ("ng", 10), ("n15", 10), ("cc", 10), ("k1", 10), ("k2", 10), ("k3", 10), ("k4", 10), ("k5", 10), ("k6", 10), ("k7", 10), ("k8", 10), ("k9", 10))),
+                ("i", (("E1", 20), ("EI", 20), ("E2", 20), ("E3", 20), ("E4", 20), ("X2", 20), ("XS", 20), ("Y2", 20), ("YS", 20), ("CI", 20), ("SI", 20), ("PJ", 80), ("PJM", 80),
+                       ("SGI", 20), ("SGJ", 20), ("T6", 100), ("IX", 100), ("KI", 80), ("KJ", 40), ("KK", 20), ("PN", 20), ("IN", 40), ("IM", 40),
+                       ("UE", 160), ("UF", 160), ("UG", 160), ("y", 10), ("code", 10), ("c5", 10), ("wi", 10), ("hh", 10), ("xi", 10), ("jh", 10), ("jl", 10),
+                       ("CCI", 1), ("CCJ", 1), ("ZA", 160), ("ZB", 160))),
+                ("b", (("EQ", 320), ("W3", 960), ("OEB", 320), ("SO", 20), ("SGH", 20), ("QD", 640), ("ZE", 320), ("X", 1280), ("XO", 320), ("NXO", 320),
+                       ("XN", 320), ("RN", 320), ("DG", 2560), ("RH", 208), ("LH", 1280), ("JHL", 20), ("JQ", 160), ("NK", 160), ("JB", 480),
+                       ("inj", 10), ("xb", 10))),
+                ("u", (("EU", 20), ("OU", 20), ("PU", 40), ("IXU", 100), ("IXN", 40), ("UI", 160), ("CU", 10)))):
+    for _n, _w in _l:
+        LOCAL.add(_n)
+        for _i in (0, 1):
+            _put(_n + "#%d" % _i, _w, _k)
+for _i in (0, 1):
+    _own("DWa%d" % _i, 832, "b")
+    _own("Ga%d" % _i, 2880, "b")
+    _own("OWa%d" % _i, 2880, "b")
+for _n, _w, _k in (("GLI", 320, "i"), ("NBI", 320, "i"), ("V8I", 640, "i"), ("RW", 4112, "b"), ("SS", 2048, "b"), ("EX", 2048, "b"), ("EH", 512, "f"),
+                   ("FLB", 2560, "b"), ("SG", 5120, "b"), ("GS", 2560, "b"), ("GL1", 336, "f"), ("YD", 320, "f"), ("GDI", 20, "b")):
+    _own(_n, _w, _k)
+for _t in range(RO):
+    _own("DX%d" % _t, 2880, "b")
+    for _n in ("CS", "CL", "GD", "GH"):
+        _own("%s%d" % (_n, _t), 20, "b")
+    _own("ZS%d" % _t, 160, "b")
+for _t in range(RO + 1):
+    _own("Z%d" % _t, 176, "b")
+for _t in range(8):
+    SCRATCH["P%d" % _t] = ("psum", [128, 512], "float32")
+    VIEW["P%d" % _t] = ("P%d" % _t, 0, 512)
+SEMAPHORES = ["sV", "sS", "sT", "sG", "loc", "ac0", "ac1", "ac2", "ag0", "ag1", "ag2", "az1", "az2", "az3",
+              "d_gl", "d_val", "d_th", "d_nb", "d_zl", "d_rec", "d_x1", "d_x2", "d_yl", "d_yd", "d_yz"]
+
+
+def rank_program(g, core, T, topo):
+    rank = T.rank_of(core)
+    if rank is None:
+        return
+    cores = list(T.cores)
+    queue = {"V": g.vector, "S": g.scalar, "T": g.tensor, "G": g, "Y": g.sync}
+    cur = [0]
+    ops = []
+    acc = {}
+
+    def c(name, lo=0, hi=None, step=1, np=128):
+        buf, o, w = VIEW[name + "#%d" % cur[0] if name in LOCAL else name]
+        return (buf, o + lo, o + (w if hi is None else hi), step, np)
+
+    def meet(a, lo, hi, step):
+        if a[1] <= lo or hi <= a[0]:
+            return False
+        return not (a[2] == step and step > 1 and a[0] % step != lo % step)
+
+    def node(q, calls, outs, ins, cost, lat=0.0, **kw):
+        r, w = [], []
+        for v in ins:
+            if isinstance(v, tuple):
+                r += [v[1], v[2]] if v[0] == "@" else [v]
+        for v in outs:
+            if v[0] == "@":
+                w.append(v[1])
+                r.append(v[2])
+            else:
+                w.append(v)
+        k, preds = len(ops), {}
+        for kind, views in ((0, r), (1, w)):
+            for (name, lo, hi, step, np) in views:
+                psum = SCRATCH[name][0] == "psum"
+                for a in acc.get(name, []):
+                    oq = ops[a[4]]["q"]
+                    if psum and oq != q:
+                        preds[a[4]] = True
+                        continue
+                    if not meet(a, lo, hi, step) or (a[3] == 0 and kind == 0):
+                        continue
+                    soft = oq == q and q == "T"
+                    preds[a[4]] = preds.get(a[4], False) or not soft
+        for (name, lo, hi, step, np) in w:
+            acc[name] = [a for a in acc.get(name, []) if not (lo <= a[0] and a[1] <= hi and step == 1 and np == 128)]
+            acc[name].append([lo, hi, step, 1, k])
+        for (name, lo, hi, step, np) in r:
+            acc.setdefault(name, []).append([lo, hi, step, 0, k])
+        d = {"q": q, "calls": calls, "preds": preds, "cost": cost, "lat": lat}
+        d.update(kw)
+        ops.append(d)
+        return k
+
+    def ap(v):
+        name, lo, hi, step, np = v
+        return T[name][0:np, lo:hi:step] if np != 128 else T[name][:, lo:hi:step]
+
+    def opnd(v):
+        if isinstance(v, tuple):
+            return ap(v[1]).indirect(ap(v[2])) if v[0] == "@" else ap(v)
+        return v
+
+    def at(win, off):
+        return ("@", win, off)
+
+    def width(v):
+        return 16 * (v[2][2] - v[2][1]) if v[0] == "@" else -(-(v[2] - v[1]) // v[3])
+
+    def size2(v):
+        return SCRATCH[(v[1] if v[0] == "@" else v)[0]][2] in ("bfloat16", "uint16")
+
+    def cyc(out, ins, two=False):
+        n = width(out)
+        if out[0] == "@":
+            return 60 + 3.0 * n
+        if any(v[0] == "@" for v in ins):
+            return 60 + 1.56 * n
+        if two:
+            return n * (1 if any(SCRATCH[v[0]][0] == "psum" for v in ins) else 2)
+        return n * (0.5 if all(size2(v) for v in [out] + ins) else 1)
+
+    def vec(call, out, ins, cy):
+        node("V", [call], [out], ins, max(64.0, cy) * 0.00104)
+
+    def tt(out, a, b, op):
+        vec(lambda: g.vector.tensor_tensor(opnd(out), opnd(a), opnd(b), op), out, [a, b], cyc(out, [a, b], True))
+
+    def ts(out, a, s1, op0, s2=None, op1=None):
+        if op1 is None:
+            vec(lambda: g.vector.tensor_scalar(opnd(out), opnd(a), opnd(s1), None, op0), out, [a, s1], cyc(out, [a]))
+        else:
+            vec(lambda: g.vector.tensor_scalar(opnd(out), opnd(a), opnd(s1), opnd(s2), op0, op1), out, [a, s1, s2], cyc(out, [a]))
+
+    def cp(out, a):
+        vec(lambda: g.vector.tensor_copy(opnd(out), opnd(a)), out, [a], cyc(out, [a]))
+
+    def act(out, a, scale=1.0, bias=0.0):
+        n = width(out)
+        cost = (78 + 1.56 * n if a[0] == "@" else 60 + n) * 0.00104
+        node("S", [lambda: g.scalar.activation(opnd(out), opnd(a), F.Copy, bias=bias, scale=scale)], [out], [a], cost)
+
+    def scan(out, d0, d1, op0, op1):
+        vec(lambda: g.vector.tensor_tensor_scan(ap(out), ap(d0), ap(d1), 0.0, op0, op1), out, [d0, d1], cyc(out, [d0, d1]))
+
+    def mms(lst):
+        calls = [lambda o=o, l=l, r=r, s=s, e=e: g.tensor.matmul(ap(o), ap(l), ap(r), s, e) for o, l, r, s, e in lst]
+        cost = sum(max(64, width(r)) * (1 if size2(r) else 4) for o, l, r, s, e in lst) * 0.0006
+        node("T", calls, [x[0] for x in lst], [x[1] for x in lst] + [x[2] for x in lst], cost)
+
+    def gps(call, out, ins, base):
+        node("G", [call], [out], ins, base + width(out) * 0.002)
+
+    def iota(v, pattern, base, cm):
+        if SCRATCH[v[0]][2] != "int32":
+            gps(lambda: g.iota(ap(v), pattern, base, cm, allow_small_or_imprecise_dtypes=True), v, [], 0.14)
+        else:
+            gps(lambda: g.iota(ap(v), pattern, base, cm), v, [], 0.14)
+
+    def const(v, x):
+        for lo in range(v[1], v[2], 720 * v[3]):
+            p = (v[0], lo, min(v[2], lo + 720 * v[3]), v[3], v[4])
+            iota(p, [[0, width(p)]], x, 0)
+
+    def select(out, a, pattern, op, base, cm):
+        gps(lambda: g.affine_select(ap(out), ap(a), pattern, op, 0.0, base, cm), out, [a], 0.18)
+
+    def dma(q, out_ap, in_ap, sem, reads, writes, lat):
+        node(q, [lambda: queue[q].dma_start(out_ap, in_ap)], writes, reads, 0.1, lat, sem=sem)
+
+    def send(dst_rank, src_rank, out_v, in_v, sem):
+        dst = cores[dst_rank % N]
+        m = topo.mask(core, dst)
+        rid, pid, _ = topo.addr(dst)
+        k = node("G", [lambda: g.remote_dma(ap(out_v), ap(in_v), T.sem[sem], T.sem.loc, pid, rid, m)], [], [in_v], 0.3,
+                 sent=len(topo.engines(core, dst)))
+        n = len(topo.engines(cores[src_rank % N], core))
+        ops.append({"q": "A", "calls": [], "preds": {k: False}, "cost": 0.0, "lat": 1.8, "sem": sem, "amount": n})
+        acc[out_v[0]] = [a for a in acc.get(out_v[0], []) if not meet(a, out_v[1], out_v[2], 1)]
+        acc[out_v[0]].append([out_v[1], out_v[2], 1, 1, len(ops) - 1])
+
+    SS = lambda b: c("SS", 128 * b, 128 * b + 128)
+    EX = lambda b: c("EX", 128 * b, 128 * b + 128)
+
+    def gather_lanes(out, src, lo, n):
+        mms([(out, SS(b), c(src, lo + b, lo + 16 * n, 16), b == 0, b == 15) for b in range(16)])
+
+    def spread(bank, src, n):
+        mms([(c(bank, b, 16 * n, 16), EX(b), src, True, True) for b in range(16)])
+
+    def half(n, par, d=0):
+        return c(n, d + 160 * par, d + 160 * par + 160)
+
+    def lists(par):
+        return c("GL1", 168 * par, 168 * par + 160)
+
+    dma("Y", ap(c("GLI")), T.gl[:, :], "d_gl", [], [c("GLI")], 2.2)
+    dma("S", ap(c("V8I", 0, 320, 1, 8)), T.val[:, :], "d_val", [], [c("V8I", 0, 320)], 1.9)
+    dma("Y", ap(c("NBI")), T.nb[:, :], "d_nb", [], [c("NBI")], 2.4)
+    dma("S", ap(c("V8I", 320, 480, 1, 8)), T.th[:, :], "d_th", [], [c("V8I", 320, 480)], 1.9)
+    dma("Y", ap(c("Z0", 0, 160)), T.zl[:, :], "d_zl", [], [c("Z0", 0, 160)], 2.5)
+    dma("Y", ap(c("RW", 0, 4096)), T.rec[:, :], "d_rec", [], [c("RW", 0, 4096)], 6.0)
+
+    ingroup = [[-16, 8], [0, 16]]
+    const(c("ALL1"), 1)
+    select(c("BLP"), c("ALL1"), ingroup, A.is_ge, 0, 1)
+    select(c("B1"), c("BLP"), [[16, 8], [0, 16]], A.is_ge, 15, -1)
+    iota(c("CM1"), [[0, 8], [1, 16]], 1, 0)
+    iota(c("LI"), [[0, 1]], 0, 1)
+    iota(c("SEL0", 0, 128, 1, 8), [[-1, 8], [0, 16]], 0, 1)
+    const(c("ONF"), 1)
+    for h in (0, 1):
+        for w in (0, 1):
+            e = 128 * (2 * h + w)
+            select(c("EH", e, e + 128), c("ONF"), [[-32, 4], [1000, 2], [-1, 16]], A.is_equal, -1000 * h - 16 * w, 1)
+    for b in range(16):
+        select(EX(b), c("ALL1"), ingroup, A.is_equal, -b, 1)
+    iota(c("TI"), [[1, 2], [32, 10]], 0, 0)
+    iota(c("TJ"), [[160, 2], [16, 10]], 2560, 0)
+    iota(c("MA1"), [[1, 2], [2, 160]], 1, 0)
+    iota(c("M1V"), [[2, 2], [4, 160]], 613, 0)
+    iota(c("V21"), [[2, 2], [4, 160]], 1, 0)
+    for i in (0, 1):
+        const(c("DWa%d" % i, 320, 512), 0)
+    for t in range(RO + 1):
+        const(c("Z%d" % t, 160, 176), 0)
+    iota(c("KC"), [[0, 10], [1, 16]], 0, 0)
+    const(c("RW", 4096, 4112), 0)
+    const(c("DX0"), 0)
+    const(c("OWa0"), 0)
+    const(c("MIN1"), -1)
+    select(c("ID"), c("ALL1"), [[-1, 128]], A.is_equal, 0, 1)
+    select(c("NTRI"), c("MIN1"), [[-16, 8], [-1, 16]], A.is_gt, 0, 1)
+    select(c("NTRI"), c("NTRI"), [[16, 8], [0, 16]], A.is_ge, 15, -1)
+    const(c("FLB"), 1)
+    const(c("FLB", 0, 2560, 16), 0)
+    iota(c("IOT", 0, 200), [[0, 10], [1, 20]], 32, 0)
+    const(c("IOT", 200, 208), 0)
+    iota(c("CJ"), [[16, 14]], 0, 0)
+    const(c("OWa1"), 0)
+    for i in (1, 0):
+        cur[0] = i
+        const(c("HF"), 0)
+        const(c("JC", 0, 20), 0)
+    dma("Y", ap(c("DX1")), ap(c("DX0")), "d_x1", [c("DX0")], [c("DX1")], 4.0)
+    dma("Y", ap(c("DX2")), ap(c("DX0")), "d_x2", [c("DX0")], [c("DX2")], 4.0)
+    const(c("GL1", 160, 168), -5)
+    const(c("GL1", 328, 336), -5)
+    for n in ("EVW", "ODW"):
+        const(c(n), 0)
+
+    tt(c("BLC"), c("CM1"), c("B1"), A.mult)
+    ts(c("LI"), c("LI"), 15, A.bitwise_and)
+    cp(c("LN"), c("LI"))
+    ts(c("LN2"), c("LN"), 2.0, A.mult)
+    ts(c("LK1"), c("LN"), 1.0, A.add)
+    ts(c("LC0"), c("LN"), -256.0, A.mult, 3680.0, A.add)
+    ts(c("LC1"), c("LC0"), BIG, A.subtract)
+    for b in range(16):
+        ts(SS(b), c("BLC"), float(b + 1), A.is_equal, 64.0, A.mult)
+
+    def names(par):
+        ts(half("NA", par), lists(par), -1.0, A.add)
+        ts(half("PB", par), half("NA", par), 1, A.bitwise_and)
+        ts(half("HA", par), half("NA", par), 1, A.arith_shift_right)
+        ts(half("AO", par), half("PB", par), 160.0, A.mult)
+        tt(half("AO", par), half("AO", par), half("HA", par), A.add)
+        cp(half("AOU", par), half("AO", par))
+
+    def keys(par, q):
+        if q == 0:
+            ts(half("CT", par), half("PB", par), -BIG, A.mult, c("LC0"), A.add)
+            tt(half("CK", par), half("CT", par), half("HA", par), A.add)
+        else:
+            ts(half("EMP", par), lists(par), 0.5, A.is_lt, -BIG, A.mult)
+            ts(half("CT", par), half("PB", par), BIG, A.mult, c("LC1"), A.add)
+            tt(half("CT", par), half("CT", par), half("EMP", par), A.add)
+            tt(half("CK", par, 320), half("CT", par), half("HA", par), A.add)
+
+    def places(par):
+        act(half("M2A", par), lists(par), 2.0, 35.0)
+        tt(half("BUI", par), half("NA", par), half("V21", par), A.mult)
+        ts(half("BUI", par), half("BUI", par), 4, A.arith_shift_right)
+        tt(half("BU", par), half("BUI", par), half("NA", par), A.add)
+        ts(half("INV", par), lists(par), 0.5, A.is_lt, 4096.0, A.mult)
+
+    for par in (0, 1):
+        ts(lists(par), c("GLI", par, 320, 2), 1.0, A.add)
+        ts(half("VAL", par), lists(par), 0.5, A.is_ge)
+    mms([(c("P7", 0, 320), c("B1"), c("VAL"), True, True)])
+    ts(c("NT"), c("P7", 0, 320), 4.0, A.mult, 4.0, A.add)
+    act(c("NS"), c("P7", 0, 320))
+    for par in (0, 1):
+        names(par)
+
+    def sizes_at_entries(split):
+        for lo, hi in ((split, 160), (160, 240), (240, 320)):
+            act(c("SG", 16 * lo, 16 * hi), at(c("NT"), c("AOU", lo, hi)))
+        if split:
+            cp(c("SG", 0, 16 * split), at(c("NT"), c("AOU", 0, split)))
+        for o in (0, 160):
+            mms([(c("P7", o, o + 160), SS(k), c("SG", 16 * o + k, 16 * o + 2560, 16), k == 0, k == 15) for k in range(16)])
+
+    def elect(q):
+        tt(c("KL"), c("P7", 0, 320), c("CK", 320 * q, 320 * q + 320), A.add)
+        v, o = c("T1"), c("KL")
+        vec(lambda: g.vector.transpose(ap(v), ap(o)), v, [o], 320)
+        for a, n, b in (("T1", 320, "R1"), ("R1", 160, "R2"), ("R2", 80, "R3"), ("R3", 40, "R4")):
+            tt(c(b), c(a, 0, n, 2), c(a, 1, n, 2), A.max)
+        mms([(c("P2", 64 + w, 84, 2), c("EH", 128 * (2 * h + w), 128 * (2 * h + w) + 128), c("R4", h, 20, 2), h == 0, h == 1)
+             for w in (0, 1) for h in (0, 1)])
+        ts(c("KB", 20 * q, 20 * q + 20), c("P2", 64, 84), 0.0, A.max)
+
+    NHP, NLP = c("P4", 192, 512), c("P2", 192, 512)
+    ts(c("NG"), c("NBI"), 320.0, A.is_ge, 352.0, A.mult)
+    ts(c("NP"), c("NBI"), 1, A.arith_shift_right)
+    tt(c("NG"), c("NG"), c("NP"), A.add)
+    ts(c("NQ"), c("NBI"), 1, A.bitwise_and)
+    ts(c("NPF"), c("NQ"), 160.0, A.mult)
+    for par in (0, 1):
+        tt(half("NCF", par), c("NG", par, 320, 2), c("NPF", par, 320, 2), A.add)
+    act(c("NH"), c("NCF"))
+    act(NHP, c("NH"))
+    tt(NLP, c("NCF"), NHP, A.subtract)
+    ts(c("SEL8", 0, 128, 1, 8), c("SEL0", 0, 128, 1, 8), 0.0, A.is_equal)
+    cp(c("R8", 0, 320, 1, 8), c("V8I", 0, 320, 1, 8))
+    ts(c("V8F", 0, 160, 1, 8), c("V8I", 320, 480, 1, 8), 1.0 / 16, A.mult)
+    cp(c("R8", 320, 480, 1, 8), c("V8F", 0, 160, 1, 8))
+    tt(c("R8", 480, 640, 1, 8), c("V8F", 0, 160, 1, 8), c("R8", 320, 480, 1, 8), A.subtract)
+    mms([(c("P0", 0, 320), c("SEL8", 0, 128, 1, 8), c("R8", 0, 320, 1, 8), True, True)])
+    mms([(c("P1", 0, 320), c("SEL8", 0, 128, 1, 8), c("R8", 320, 640, 1, 8), True, True)])
+    for par in (0, 1):
+        act(c("DWa0", 160 * par, 160 * par + 160), c("P0", par, 320, 2), 1.0 / 1024)
+    act(c("THL"), c("P1", 0, 320))
+    gather_lanes(c("P2", 0, 20), "DWa0", 0, 20)
+    cp(c("GDI"), c("P2", 0, 20))
+    cp(c("SO"), c("P2", 0, 20))
+    cp(c("PJM", 0, 20), c("P2", 0, 20))
+    send(rank - 1, rank + 1, c("GH0"), c("GDI"), "ag0")
+    gather_lanes(c("P2", 32, 52), "THL", 0, 20)
+    act(c("TH2"), c("P2", 32, 52))
+    tt(c("th64"), c("TH2", 0, 10), c("TH2", 10, 20), A.add)
+    ts(c("thr"), c("th64"), 15.0, A.add)
+    ts(c("AC"), c("TI"), c("LN2"), A.add)
+    ts(c("DMP"), c("TJ"), c("LN"), A.add)
+    ts(c("A21"), c("AC"), 2.0, A.mult, 1.0, A.add)
+    ts(c("CM40", 0, 20), c("AC"), 2.0, A.mult, 37.0, A.add)
+    ts(c("CM40", 20, 40), c("AC"), 2.0, A.mult, 613.0, A.add)
+    ts(c("EVW", 0, 128, 2), c("B1", 0, 128, 2), 1.0 / 512, A.mult)
+    ts(c("ODW", 1, 128, 2), c("B1", 1, 128, 2), 1.0 / 512, A.mult)
+    ts(c("FL"), c("KC"), 0.5, A.is_ge)
+    ts(c("K15"), c("KC"), -1.0, A.mult, 15.0, A.add)
+    ts(c("K10"), c("KC"), 1024.0, A.mult)
+    ts(c("CJ"), c("CJ"), c("LN"), A.add)
+    ts(c("CJ"), c("CJ"), 3277.0, A.mult)
+    ts(c("CJ"), c("CJ"), 16, A.arith_shift_right)
+    cp(c("COFF"), c("CJ"))
+
+    sizes_at_entries(60)
+    for par in (0, 1):
+        keys(par, 0)
+    elect(0)
+
+    def prep(t):
+        par = t & 1
+        cur[0] = par
+        ts(c("E1"), c("KB", 20 * par, 20 * par + 20), 160.0, A.add)
+        ts(c("EI"), c("E1"), 255, A.bitwise_and)
+        cp(c("EU"), c("EI"))
+        tt(c("EQ"), at(c("GL1", 168 * par, 168 * par + 168), c("EU")), c("MA1"), A.is_equal)
+        tt(c("W3", 0, 320), c("EQ"), NHP, A.mult)
+        tt(c("W3", 320, 640), c("EQ"), NLP, A.mult)
+        ts(c("W3", 640, 960), c("EQ"), c("LK1"), A.mult)
+        gather_lanes(c("P6", 0, 60), "W3", 0, 60)
+        ts(c("X1"), c("EI"), 4.0, A.mult, 2.0 * par + 1.0, A.add)
+        tt(c("X2"), c("AC"), c("X1"), A.mult)
+        ts(c("XS"), c("X2"), 4, A.arith_shift_right)
+        ts(c("MM2", 0, 20), c("EI"), 4.0, A.mult, 2.0 * par + 613.0, A.add)
+        tt(c("BB2", 0, 20), c("XS"), c("AC"), A.add)
+        ts(c("X6"), c("EI"), 16.0, A.mult, -1.0, A.add)
+        ts(c("E3"), c("EI"), 15, A.bitwise_and)
+        ts(c("E4"), c("EI"), 4, A.arith_shift_right)
+        ts(c("X7"), c("E3"), 160.0, A.mult, -1.0, A.add)
+        ts(c("X4"), c("E4"), 16.0, A.mult)
+        tt(c("X7"), c("X7"), c("X4"), A.add)
+        ts(c("A3"), c("P6", 0, 60), 1.0 / 64, A.mult)
+        tt(c("CI"), c("A3", 0, 20), c("A3", 20, 40), A.add)
+        cp(c("OU"), c("CI"))
+        ts(c("X3"), c("CI"), 512.0, A.is_ge, 704.0, A.mult)
+        ts(c("E2"), c("CI"), 511, A.bitwise_and)
+        ts(c("X5"), c("E2"), 160.0, A.is_ge, 319.0, A.mult)
+        tt(c("X3"), c("X3"), c("X5"), A.add)
+        ts(c("X5"), c("CI"), 2.0, A.mult)
+        tt(c("OF"), c("X5"), c("X3"), A.subtract)
+        tt(c("Y2"), c("OF"), c("A21"), A.mult)
+        ts(c("MM2", 20, 40), c("OF"), 2.0, A.mult, 37.0, A.add)
+        ts(c("YS"), c("Y2"), 4, A.arith_shift_right)
+        tt(c("BB2", 20, 40), c("YS"), c("OF"), A.add)
+        ts(c("NM"), c("A3", 40, 60), 0.5, A.is_lt)
+        tt(c("DN"), c("NM"), c("DMP"), A.mult)
+        for j in (1, 2, 3):
+            act(c("JC", 20 * j, 20 * j + 20), c("NM"), BIG, 16.0 * j)
+        for j, x in ((0, "X6"), (20, "X7")):
+            tt(c(x), c(x), c("A3", 40, 60), A.add)
+            tt(c("PX", j, j + 20), c(x), c("DN"), A.max)
+        cp(c("PU"), c("PX"))
+        ow = "OWa%d" % par
+        mms([(c("P6", 128, 448), c("EVW"), c("W3", 0, 320), True, False), (c("P6", 128, 448), c("ODW"), c("W3", 320, 640), False, True)])
+        act(c("OEB"), c("P6", 128, 448))
+        cp(at(c(ow), c("PU", 20, 40)), c("OEB"))
+        mms([(c("P7", 320, 480), SS(b), c(ow, 160 * b, 160 * b + 160), b == 0, False) for b in range(16)]
+            + [(c("P7", 320, 480), c("ID"), c("K10"), False, True)])
+        cur[0] = 1 - par
+
+    prep(0)
+    for par in (0, 1):
+        keys(par, 1)
+    elect(1)
+    cur[0] = 0
+    places(0)
+    places(1)
+
+    for t in range(RO):
+        par = t & 1
+        po = 160 * par
+        cur[0] = par
+        zw = "Z%d" % t
+        dw = "DWa%d" % par
+        if t:
+            cur[0] = 1 - par
+            pn = c("PN")
+            cur[0] = par
+            tt(c("SGI"), c("GH%d" % t), c("P6", 64, 84), A.add)
+            ts(c("SGJ"), c("SGI"), 15, A.bitwise_and)
+            cp(c("SGH"), c("SGJ"))
+            spread("P1", c("SGH"), 20)
+            act(c(dw, 512, 832), c("P1", 0, 320), 1.0 / 1024)
+            tt(c("SI"), pn, c("CL%d" % (t - 1)), A.add)
+            ts(c("PJM", 0, 20), c("SI"), 15, A.bitwise_and)
+            cp(c("SO"), c("PJM", 0, 20))
+            spread("P0", c("SO"), 20)
+            ts(c(dw, 0, 320), c("P0", 0, 320), 1.0 / 1024, A.mult)
+        else:
+            spread("P1", c("GH0"), 20)
+            act(c(dw, 512, 832), c("P1", 0, 320), 1.0 / 1024)
+            spread("P0", c("SO"), 20)
+        cp(c("QD", 0, 320), at(c(dw, po, po + 176), c("EU")))
+        act(c("QD", 320, 640), at(c(dw), c("OU")))
+        gather_lanes(c("P2", 0, 40), "QD", 0, 40)
+        for j in (1, 2, 3):
+            ts(c("PJ", 20 * j, 20 * j + 20), c("PJM", 0, 20), float(j), A.add)
+        ts(c("PJM", 20, 80), c("PJ", 20, 80), 15, A.bitwise_and)
+        for j in range(4):
+            tt(c("TP", 20 * j, 20 * j + 20), c("PJM", 20 * j, 20 * j + 20), c("MM2", 0, 20), A.mult)
+        tt(c("TP", 80, 100), c("PJM", 0, 20), c("MM2", 20, 40), A.mult)
+        tt(c("J2"), c("JC"), c("PJM"), A.add)
+        tt(c("U"), c("P2", 0, 40), c("CM40"), A.mult)
+        tt(c("B40"), c("BB2"), c("U"), A.add)
+        for j in range(5):
+            tt(c("T6", 20 * j, 20 * j + 20), c("TP", 20 * j, 20 * j + 20), c("B40", j // 4 * 20, j // 4 * 20 + 20), A.add)
+        ts(c("IX"), c("T6"), 4095, A.bitwise_and)
+        cp(c("IXU"), c("IX"))
+        act(c("ZE"), at(c(zw), c("EU")))
+        for j in range(4):
+            tt(c("X", 320 * j, 320 * j + 320), at(c("RW", 0, 4096), c("IXU", 20 * j, 20 * j + 20)), c("ZE"), A.max)
+        gather_lanes(c("P3", 0, 80), "X", 0, 80)
+        for hf in (0, 80):
+            act(c("DG", 16 * hf, 16 * hf + 1280), at(c(dw, 0, 320), c("AOU", po + hf, po + hf + 80)))
+        mms([(c("P4", 0, 160), SS(k), c("DG", k, 2560, 16), k == 0, k == 15) for k in range(16)])
+        tt(c("P0", 320, 480), half("M2A", par), c("P0", po, po + 160), A.mult)
+        tt(c("UC"), half("BU", par), c("P0", 320, 480), A.add)
+        tt(c("P3", 320, 480), half("M1V", par), c("P4", 0, 160), A.mult)
+        tt(c("UE"), c("UC"), c("P3", 320, 480), A.add)
+        ts(c("UF"), c("UE"), 4095, A.bitwise_and)
+        tt(c("UG"), c("UF"), half("INV", par), A.max)
+        cp(c("UI"), c("UG"))
+        gw = "Ga%d" % par
+        tt(c("XO"), at(c("RW", 0, 4096), c("IXU", 80, 100)), c("ZE"), A.max)
+        act(c("NXO"), c("XO"), -1.0)
+        tt(c("KI"), c("P3", 0, 80), c("J2"), A.add)
+        tt(c("KJ"), c("KI", 0, 40), c("KI", 40, 80), A.min)
+        tt(c("KK"), c("KJ", 0, 20), c("KJ", 20, 40), A.min)
+        ts(c("PN"), c("KK"), 15, A.bitwise_and)
+        tt(c("PQ", 20, 40), c("PN"), c("MM2", 20, 40), A.mult)
+        tt(c("PQ", 0, 20), c("PN"), c("MM2", 0, 20), A.mult)
+        tt(c("IN"), c("PQ"), c("B40"), A.add)
+        ts(c("IM"), c("IN"), 4095, A.bitwise_and)
+        cp(c("IXN"), c("IM"))
+        if t < RO - 1:
+            cp(c("GD%d" % t), c("PN"))
+            send(rank - 1, rank + 1, c("GH%d" % (t + 1)), c("GD%d" % t), "ag%d" % (t + 1))
+        tt(c("XN"), at(c("RW", 0, 4096), c("IXN", 20, 40)), c("ZE"), A.max)
+        tt(at(c("DX%d" % t), c("PU", 20, 40)), c("XN"), c("NXO"), A.add)
+        mms([(c("P5", 0, 160), SS(b), c("DX%d" % t, 160 * b, 160 * b + 160), b == 0, False) for b in range(16)]
+            + [(c("P5", 0, 160), c("ID"), c("K15"), False, True)])
+        act(c("RN"), at(c("RW", 0, 4096), c("IXN", 0, 20)))
+        for hf in (0, 80):
+            act(c(gw, 16 * hf, 16 * hf + 1280), at(c("RW"), c("UI", hf, hf + 80)))
+        scan(c("S1"), c("FL"), c("P5", 0, 160), A.mult, A.max)
+        tt(c("QE"), c("S1"), c("P5", 0, 160), A.is_equal)
+        tt(c("QY"), c("QE"), c("P7", 320, 480), A.mult)
+        scan(c("S2"), c("FL"), c("QY"), A.mult, A.max)
+        tt(c("inj"), c("S1", 15, 160, 16), c("thr"), A.is_gt)
+        cp(c("y"), c("S2", 15, 160, 16))
+        ts(c("code"), c("y"), 1023, A.bitwise_and)
+        ts(c("gh"), c("code"), 512.0, A.is_ge)
+        tt(c("xb"), c("inj"), c("gh"), A.mult)
+        mms([(c("P5", 192, 202), c("B1"), c("xb"), True, True), (c("P5", 208, 218), c("NTRI"), c("xb"), True, True)])
+        ts(c("wi"), c("code"), 15, A.bitwise_and)
+        ts(c("w"), c("wi"), 1.0, A.add)
+        ts(c("hh"), c("code"), 4, A.arith_shift_right)
+        for x in range(10):
+            ts(c("LH", 128 * x, 128 * x + 128), c("BLC"), c("w", x, x + 1), A.is_equal)
+        tt(c("xh"), c("xb"), c("hh"), A.mult)
+        scan(c("cs"), c("ONF", 0, 10), c("P5", 192, 202), A.mult, A.add)
+        tt(c("pre"), c("cs"), c("P5", 208, 218), A.add)
+        ts(c("prf"), c("pre"), float(CAP), A.is_le)
+        tt(c("HF", 0, 10), c("prf"), c("xh"), A.mult)
+        tt(c("RH"), at(c("HF"), c("COFF", 0, 13)), c("IOT"), A.is_equal)
+        mms([(c("P6", 64, 84), c("LH", 128 * x, 128 * x + 128), c("RH", 20 * x, 20 * x + 20), x == 0, x == 9) for x in range(10)])
+        cp(c("CS%d" % t), c("P6", 64, 84))
+        send(rank + 1, rank - 1, c("CL%d" % t), c("CS%d" % t), "ac%d" % t)
+        cp(at(c(gw), c("PU", 0, 20)), c("RN"))
+        scan(c("GS"), c("FLB"), c(gw, 0, 2560), A.mult, A.max)
+        tt(c("ZA"), c(zw, 0, 160), c("GS", 15, 2560, 16), A.add)
+        ts(c("ZB"), c("ZA"), 1, A.arith_shift_right)
+        cp(c("ZS%d" % t), c("ZB"))
+        send(rank + 1 + t, rank - 1 - t, c("Z%d" % (t + 1), 0, 160), c("ZS%d" % t), "az%d" % (t + 1))
+        l1, ns, last = lists(par), half("NS", par), t == RO - 1
+        ts(c("NK"), ns, c("LN"), A.is_equal)
+        act(c("JB", 160, 320), ns)
+        gather_lanes(c("P2", 144, 154), "JB", 160, 10)
+        ts(c("n15"), c("P2", 144, 154), 15.5 * 1024, A.is_le)
+        ts(c("ng"), c("gh"), 0.5, A.is_lt)
+        tt(c("cc"), c("inj"), c("n15"), A.mult)
+        tt(c("cd"), c("cc"), c("ng"), A.mult)
+        ts(c("c5"), c("code"), 511, A.bitwise_and)
+        ts(c("pu"), c("c5"), 160.0, A.is_ge)
+        ts(c("k1"), c("pu"), -319.0, A.mult, 1.0, A.add)
+        ts(c("oo"), c("c5"), 2.0, A.mult)
+        tt(c("op"), c("oo"), c("k1"), A.add)
+        tt(c("xi"), c("op"), c("cd"), A.mult)
+        ts(c("jh"), c("xi"), 496, A.bitwise_and)
+        ts(c("jl"), c("xi"), 15, A.bitwise_and)
+        cp(c("JHL", 0, 10), c("jh"))
+        cp(c("JHL", 10, 20), c("jl"))
+        mms([(c("P1", b, 160, 16), EX(b), c("JHL", 10 * h, 10 * h + 10), h == 0, h == 1) for b in range(16) for h in (0, 1)])
+        tt(c("JQ"), l1, c("P1", 0, 160), A.is_equal)
+        mms([(c("P3", 128, 288), c("B1"), c("JQ"), True, True)])
+        if not last:
+            cp(c("CU"), c("c5"))
+            cp(c("JB", 0, 160), at(c("NT"), c("CU")))
+        ts(c("JA"), c("P3", 128, 288), 0.5, A.is_lt)
+        jv, jw = c("P1", 160, 320), c("P1", 320, 480)
+        tt(jv, c("JA"), c("P1", 0, 160), A.mult)
+        if not last:
+            ts(c("JB", 320, 480), jv, 0.5, A.is_ge)
+            gather_lanes(c("P2", 96, 126), "JB", 0, 30)
+        tt(jw, c("NK"), jv, A.mult)
+        tt(l1, l1, jw, A.add)
+        ts(c("YL", par, 320, 2), l1, -1.0, A.add)
+        if not last:
+            if t == 0:
+                tt(ns, ns, c("JB", 320, 480), A.add)
+            act(c("J3"), c("P2", 96, 126))
+            ts(c("k2"), c("J3", 10, 20), -0.25, A.mult, 3680.0, A.add)
+            ts(c("k3"), c("pu"), -160.0, A.mult)
+            tt(c("k5"), c("k3"), c("c5"), A.add)
+            ts(c("k4"), c("pu"), float(1 - par), A.is_equal, 1.0 / 1024, A.mult)
+            tt(c("k6"), c("k2"), c("J3", 0, 10), A.add)
+            tt(c("k7"), c("k6"), c("k5"), A.add)
+            tt(c("k8"), c("k4"), c("J3", 20, 30), A.mult)
+            tt(c("k9"), c("k7"), c("k8"), A.mult)
+            kb = c("KB", 20 * (1 - par) + 10 * par, 20 * (1 - par) + 10 * par + 10)
+            tt(kb, kb, c("k9"), A.max)
+            mms([(c("P5", 224, 234), c("ALL1"), c("inj"), True, True)])
+            o, i = c("CC", 0, 1), c("P5", 224, 234)
+            vec(lambda o=o, i=i: g.vector.tensor_reduce(ap(o), ap(i), AxisListType.X, A.add), o, [i], 10)
+            cp(c("CCI"), o)
+            ts(c("CCJ"), c("CCI"), 31, A.bitwise_and)
+            ts(c("CC", 1, 2), c("CCJ"), 64.0, A.mult, 15.0, A.add)
+            inc = c("CC", 1, 2)
+            cur[0] = 1 - par
+            ts(c("thr"), c("th64"), inc, A.add)
+            prep(t + 1)
+            if t == 0:
+                cur[0] = 0
+                ts(c("NT", 0, 160), c("NS", 0, 160), 4.0, A.mult, 4.0, A.add)
+                names(0)
+                keys(0, 0)
+                places(0)
+                sizes_at_entries(0)
+                elect(0)
+
+    cur[0] = (RO - 1) & 1
+    pn = c("PN")
+    dma("Y", T.yl[:, :], ap(c("YL")), "d_yl", [c("YL")], [], 2.2)
+    cur[0] = RO & 1
+    tt(c("SI"), pn, c("CL%d" % (RO - 1)), A.add)
+    cp(c("SO"), c("SI"))
+    spread("P0", c("SO"), 20)
+    cp(c("YDI"), c("P0", 0, 320))
+    ts(c("YDJ"), c("YDI"), 15, A.bitwise_and)
+    for par in (0, 1):
+        cp(c("YD", par, 320, 2), half("YDJ", par))
+    dma("S", T.yd[:, :], T["YD"][0:128:16, :], "d_yd", [c("YD")], [], 2.0)
+    dma("Y", T.yz[:, :], ap(c("Z%d" % RO, 0, 160)), "d_yz", [c("Z%d" % RO, 0, 160)], [], 2.2)
+
+    succ = [[] for _ in ops]
+    for k, d in enumerate(ops):
+        for p in d["preds"]:
+            succ[p].append(k)
+    prio = [0.0] * len(ops)
+    for k in range(len(ops) - 1, -1, -1):
+        d = ops[k]
+        prio[k] = d["cost"] + d["lat"] + max([prio[s] + 0.06 for s in succ[k]], default=0.0)
+    left = [len(d["preds"]) for d in ops]
+    ready = [0.0] * len(ops)
+    pool = {q: [] for q in "VSTGYA"}
+    for k, d in enumerate(ops):
+        if not left[k]:
+            pool[d["q"]].append(k)
+    free = {q: 0.0 for q in pool}
+    order = []
+    while len(order) < len(ops):
+        best = None
+        for q in pool:
+            for k in pool[q]:
+                s = ready[k] if q == "A" else max(free[q], ready[k])
+                key = (s, -prio[k], k)
+                if best is None or key < best[0]:
+                    best = (key, q, k)
+        (s, _, k), q, _ = best
+        pool[q].remove(k)
+        d = ops[k]
+        free[q] = s + d["cost"] + 0.012
+        end = s + d["cost"] + d["lat"]
+        order.append(k)
+        for x in succ[k]:
+            gap = 0.06 if ops[x]["preds"][k] else 0.0
+            ready[x] = max(ready[x], end + gap)
+            left[x] -= 1
+            if not left[x]:
+                pool[ops[x]["q"]].append(x)
+
+    count = {q: 0 for q in "VSTG"}
+    clock = {q: {} for q in "VSTGY"}
+    token = [None] * len(ops)
+    sent = 0
+    for k in order:
+        d = ops[k]
+        q = d["q"]
+        if q == "A":
+            token[k] = (d["sem"], d["amount"], {d["sem"]: d["amount"]})
+            continue
+        ck, best = clock[q], {}
+        for p, hard in d["preds"].items():
+            if hard:
+                s, v, kk = token[p]
+                if ck.get(s, 0) < v and best.get(s, (0, None))[0] < v:
+                    best[s] = (v, kk)
+        for s in list(best):
+            v = best[s][0]
+            if any(s2 != s and k2.get(s, 0) >= v for s2, (v2, k2) in best.items()):
+                del best[s]
+        for s, (v, kk) in best.items():
+            queue[q].wait_ge(T.sem[s], v)
+            for s2, v2 in kk.items():
+                ck[s2] = max(ck.get(s2, 0), v2)
+        for call in d["calls"]:
+            if "sem" in d:
+                call().then_inc(T.sem[d["sem"]], 16)
+            elif "sent" in d:
+                call()
+                sent += d["sent"]
+            else:
+                count[q] += 1
+                call().then_inc(T.sem["s" + q], 1)
+        kk = dict(ck)
+        if "sem" in d:
+            kk[d["sem"]] = 16
+            token[k] = (d["sem"], 16, kk)
+        elif "sent" not in d:
+            kk["s" + q] = count[q]
+            token[k] = ("s" + q, count[q], kk)
+    g.wait_ge(T.sem.loc, sent)
+    for s in ("d_yl", "d_yd", "d_yz"):
+        g.wait_ge(T.sem[s], 16)
+    for q in "VSTG":
+        if clock["G"].get("s" + q, 0) < count[q]:
+            g.wait_ge(T.sem["s" + q], count[q])

@@ -25,26 +25,27 @@ def _put(name, width, kind):
 for _n, _w in (("BLP", 128), ("CM1", 128), ("B1", 128), ("BLC", 128), ("ALL1", 128), ("MIN1", 128), ("NTRI", 128), ("EVW", 128), ("ODW", 128), ("ID", 128),
                ("VAL", 320), ("NT", 320), ("NH", 320), ("R8", 640), ("SEL8", 128), ("THL", 320), ("SEL0", 128), ("K15", 160), ("K10", 160)):
     _put(_n, _w, "b")
-for _n, _w in (("ONF", 128), ("LN", 1), ("LN2", 1), ("LK1", 1), ("LC0", 1), ("LC1", 1), ("AC", 20), ("DMP", 20), ("A21", 20), ("CM40", 40),
-               ("MA1", 320), ("M1V", 320), ("V21", 320), ("KC", 160), ("FL", 160), ("IOT", 208),
-               ("AO", 320), ("M2A", 320), ("BU", 320), ("INV", 320), ("CT", 320), ("CK", 640), ("NS", 320), ("KB", 40),
-               ("NG", 320), ("NPF", 320), ("NCF", 320), ("V8F", 160), ("TH2", 20), ("th64", 10), ("YL", 320), ("EMP", 320)):
+for _n, _w in (("ONF", 128), ("LN", 1), ("LN2", 1), ("LNB", 1), ("LNC", 1), ("LNN", 1), ("ON1", 1), ("LK1", 1), ("LC0", 1), ("LC1", 1),
+               ("AC", 20), ("DMP", 20), ("A21", 20), ("CM40", 40),
+               ("MA1", 320), ("M1V", 320), ("V21", 320), ("KC", 320), ("FL", 320), ("IOT", 208),
+               ("AO", 320), ("HA", 320), ("M2A", 320), ("BU", 320), ("INV", 320), ("CT", 320), ("CK", 640), ("NS", 320), ("KB", 40),
+               ("NCF", 320), ("V8F", 160), ("TH2", 20), ("th64", 10), ("YL", 320), ("EMP", 320)):
     _put(_n, _w, "f")
-for _n, _w in (("LI", 1), ("TI", 20), ("TJ", 20), ("CJ", 14), ("NA", 320), ("PB", 320), ("HA", 320), ("BUI", 320), ("NP", 320), ("NQ", 320), ("YDI", 320), ("YDJ", 320)):
+for _n, _w in (("LI", 1), ("TI", 20), ("TJ", 20), ("CJ", 14), ("NA", 320), ("PB", 320), ("BUI", 320)):
     _put(_n, _w, "i")
 for _n, _w in (("AOU", 320), ("COFF", 14)):
     _put(_n, _w, "u")
 LOCAL = set()
-for _k, _l in (("f", (("T1", 320), ("KL", 320), ("R1", 160), ("R2", 80), ("R3", 40), ("R4", 20), ("A3", 60), ("X1", 20), ("X3", 20), ("X4", 20), ("X5", 20),
-                      ("X6", 20), ("X7", 20), ("OF", 20), ("NM", 20), ("DN", 20), ("PX", 40), ("MM2", 40), ("BB2", 40), ("JC", 80), ("J2", 80), ("TP", 100),
+for _k, _l in (("f", (("T1", 320), ("KL", 320), ("R1", 320), ("A3", 60), ("X1", 20), ("X3", 20), ("X4", 20), ("X5", 20),
+                      ("X6", 20), ("X7", 20), ("X8", 20), ("OF", 20), ("NM", 20), ("DN", 20), ("PX", 40), ("MM2", 40), ("BB2", 40), ("JC", 80), ("J2", 80), ("TP", 100),
                       ("U", 40), ("B40", 40), ("PQ", 40), ("UC", 160), ("S1", 160), ("QE", 160), ("QY", 160), ("S2", 160), ("HF", 16),
-                      ("CC", 2), ("JA", 160), ("J3", 30),
-                      ("thr", 10), ("gh", 10), ("xh", 10), ("cs", 10), ("pre", 10), ("prf", 10), ("w", 10), ("cd", 10), ("pu", 10), ("oo", 10), ("op", 10),
-                      ("ng", 10), ("n15", 10), ("cc", 10), ("k1", 10), ("k2", 10), ("k3", 10), ("k4", 10), ("k5", 10), ("k6", 10), ("k7", 10), ("k8", 10), ("k9", 10))),
-                ("i", (("E1", 20), ("EI", 20), ("E2", 20), ("E3", 20), ("E4", 20), ("X2", 20), ("XS", 20), ("Y2", 20), ("YS", 20), ("CI", 20), ("SI", 20), ("PJ", 80), ("PJM", 80),
-                       ("SGI", 20), ("SGJ", 20), ("T6", 100), ("IX", 100), ("KI", 80), ("KJ", 40), ("KK", 20), ("PN", 20), ("IN", 40), ("IM", 40),
-                       ("UE", 160), ("UF", 160), ("UG", 160), ("y", 10), ("code", 10), ("c5", 10), ("wi", 10), ("hh", 10), ("xi", 10), ("jh", 10), ("jl", 10),
-                       ("CCI", 1), ("CCJ", 1), ("ZA", 160), ("ZB", 160))),
+                      ("CC", 2), ("JA", 160), ("J3", 30), ("NKA", 160), ("p10", 10), ("p16", 10),
+                      ("thr", 10), ("gh", 10), ("xh", 10), ("cs", 10), ("pre", 10), ("prf", 10), ("w", 10), ("cd", 10), ("op", 10),
+                      ("ng", 10), ("n15", 10), ("cc", 10), ("k1", 10), ("k2", 10), ("k4", 10), ("k6", 10), ("k7", 10), ("k8", 10), ("k9", 10))),
+                ("i", (("E1", 20), ("EI", 20), ("E2", 20), ("E3", 20), ("E4", 20), ("X2", 20), ("XS", 20), ("Y2", 20), ("YS", 20), ("CI", 20), ("CS1", 20), ("SI", 20),
+                       ("PJ", 80), ("PJM", 80), ("SGI", 20), ("SGJ", 20), ("T6", 100), ("IX", 100), ("KI", 80), ("KJ", 40), ("KK", 20), ("PN", 20), ("IN", 40), ("IM", 40),
+                       ("UE", 160), ("UF", 160), ("UG", 160), ("y", 10), ("code", 10), ("wi", 10), ("pb", 10), ("h5", 10), ("o2", 10), ("hh", 10),
+                       ("xi", 10), ("jh", 10), ("jl", 10), ("CCI", 1), ("CCJ", 1), ("ZA", 160), ("ZB", 160))),
                 ("b", (("EQ", 320), ("W3", 960), ("OEB", 320), ("SO", 20), ("SGH", 20), ("QD", 640), ("ZE", 320), ("X", 1280), ("XO", 320), ("NXO", 320),
                        ("XN", 320), ("RN", 320), ("DG", 2560), ("RH", 208), ("LH", 1280), ("JHL", 20), ("JQ", 160), ("NK", 160), ("JB", 480),
                        ("inj", 10), ("xb", 10))),
@@ -62,7 +63,7 @@ for _n, _w, _k in (("GLI", 320, "i"), ("NBI", 320, "i"), ("V8I", 640, "i"), ("RW
     _own(_n, _w, _k)
 for _t in range(RO):
     _own("DX%d" % _t, 2880, "b")
-    for _n in ("CS", "CL", "GD", "GH"):
+    for _n in ("CN", "CL", "GD", "GH"):
         _own("%s%d" % (_n, _t), 20, "b")
     _own("ZS%d" % _t, 160, "b")
 for _t in range(RO + 1):
@@ -71,7 +72,7 @@ for _t in range(8):
     SCRATCH["P%d" % _t] = ("psum", [128, 512], "float32")
     VIEW["P%d" % _t] = ("P%d" % _t, 0, 512)
 SEMAPHORES = ["sV", "sS", "sT", "sG", "loc", "ac0", "ac1", "ac2", "ag0", "ag1", "ag2", "az1", "az2", "az3",
-              "d_gl", "d_val", "d_th", "d_nb", "d_zl", "d_rec", "d_x1", "d_x2", "d_yl", "d_yd", "d_yz"]
+              "d_gl", "d_val", "d_th", "d_nb", "d_zl", "d_rec", "d_x1", "d_x2", "d_o0", "d_o1", "d_yl", "d_yd", "d_yz"]
 
 
 def rank_program(g, core, T, topo):
@@ -170,10 +171,10 @@ def rank_program(g, core, T, topo):
     def cp(out, a):
         vec(lambda: g.vector.tensor_copy(opnd(out), opnd(a)), out, [a], cyc(out, [a]))
 
-    def act(out, a, scale=1.0, bias=0.0):
+    def act(out, a, scale=1.0, bias=0.0, func=F.Copy):
         n = width(out)
         cost = (78 + 1.56 * n if a[0] == "@" else 60 + n) * 0.00104
-        node("S", [lambda: g.scalar.activation(opnd(out), opnd(a), F.Copy, bias=bias, scale=scale)], [out], [a], cost)
+        node("S", [lambda: g.scalar.activation(opnd(out), opnd(a), func, bias=opnd(bias), scale=opnd(scale))], [out], [a, bias, scale], cost)
 
     def scan(out, d0, d1, op0, op1):
         vec(lambda: g.vector.tensor_tensor_scan(ap(out), ap(d0), ap(d1), 0.0, op0, op1), out, [d0, d1], cyc(out, [d0, d1]))
@@ -259,26 +260,25 @@ def rank_program(g, core, T, topo):
         const(c("DWa%d" % i, 320, 512), 0)
     for t in range(RO + 1):
         const(c("Z%d" % t, 160, 176), 0)
-    iota(c("KC"), [[0, 10], [1, 16]], 0, 0)
+    iota(c("KC"), [[0, 20], [1, 16]], 0, 0)
     const(c("RW", 4096, 4112), 0)
-    const(c("DX0"), 0)
-    const(c("OWa0"), 0)
+    zero = c("DX0")
+    vec(lambda: g.vector.memset(ap(zero), 0.0), zero, [], 1440)
     const(c("MIN1"), -1)
     select(c("ID"), c("ALL1"), [[-1, 128]], A.is_equal, 0, 1)
     select(c("NTRI"), c("MIN1"), [[-16, 8], [-1, 16]], A.is_gt, 0, 1)
     select(c("NTRI"), c("NTRI"), [[16, 8], [0, 16]], A.is_ge, 15, -1)
     const(c("FLB"), 1)
     const(c("FLB", 0, 2560, 16), 0)
-    iota(c("IOT", 0, 200), [[0, 10], [1, 20]], 32, 0)
+    iota(c("IOT", 0, 200), [[0, 10], [1, 20]], 10, 0)
     const(c("IOT", 200, 208), 0)
     iota(c("CJ"), [[16, 14]], 0, 0)
-    const(c("OWa1"), 0)
     for i in (1, 0):
         cur[0] = i
         const(c("HF"), 0)
         const(c("JC", 0, 20), 0)
-    dma("Y", ap(c("DX1")), ap(c("DX0")), "d_x1", [c("DX0")], [c("DX1")], 4.0)
-    dma("Y", ap(c("DX2")), ap(c("DX0")), "d_x2", [c("DX0")], [c("DX2")], 4.0)
+    for n, s in (("OWa0", "d_o0"), ("OWa1", "d_o1"), ("DX1", "d_x1"), ("DX2", "d_x2")):
+        dma("Y", ap(c(n)), ap(c("DX0")), s, [c("DX0")], [c(n)], 4.0)
     const(c("GL1", 160, 168), -5)
     const(c("GL1", 328, 336), -5)
     for n in ("EVW", "ODW"):
@@ -288,6 +288,10 @@ def rank_program(g, core, T, topo):
     ts(c("LI"), c("LI"), 15, A.bitwise_and)
     cp(c("LN"), c("LI"))
     ts(c("LN2"), c("LN"), 2.0, A.mult)
+    const(c("LNB"), 4096)
+    const(c("LNC"), int(BIG))
+    const(c("ON1"), 1)
+    ts(c("LNN"), c("LN"), -1.0, A.mult)
     ts(c("LK1"), c("LN"), 1.0, A.add)
     ts(c("LC0"), c("LN"), -256.0, A.mult, 3680.0, A.add)
     ts(c("LC1"), c("LC0"), BIG, A.subtract)
@@ -297,19 +301,19 @@ def rank_program(g, core, T, topo):
     def names(par):
         ts(half("NA", par), lists(par), -1.0, A.add)
         ts(half("PB", par), half("NA", par), 1, A.bitwise_and)
-        ts(half("HA", par), half("NA", par), 1, A.arith_shift_right)
-        ts(half("AO", par), half("PB", par), 160.0, A.mult)
+        act(half("HA", par), lists(par), 0.5, -0.5)
+        ts(half("AO", par), half("PB", par), 159.5, A.mult)
         tt(half("AO", par), half("AO", par), half("HA", par), A.add)
         cp(half("AOU", par), half("AO", par))
 
     def keys(par, q):
         if q == 0:
-            ts(half("CT", par), half("PB", par), -BIG, A.mult, c("LC0"), A.add)
+            ts(half("CT", par), half("PB", par), -BIG - 0.5, A.mult, c("LC0"), A.add)
             tt(half("CK", par), half("CT", par), half("HA", par), A.add)
         else:
-            ts(half("EMP", par), lists(par), 0.5, A.is_lt, -BIG, A.mult)
-            ts(half("CT", par), half("PB", par), BIG, A.mult, c("LC1"), A.add)
-            tt(half("CT", par), half("CT", par), half("EMP", par), A.add)
+            act(half("EMP", par), lists(par), -BIG, c("LNC"), F.Relu)
+            ts(half("CT", par), half("PB", par), BIG - 0.5, A.mult, c("LC1"), A.add)
+            tt(half("CT", par), half("CT", par), half("EMP", par), A.subtract)
             tt(half("CK", par, 320), half("CT", par), half("HA", par), A.add)
 
     def places(par):
@@ -317,11 +321,11 @@ def rank_program(g, core, T, topo):
         tt(half("BUI", par), half("NA", par), half("V21", par), A.mult)
         ts(half("BUI", par), half("BUI", par), 4, A.arith_shift_right)
         tt(half("BU", par), half("BUI", par), half("NA", par), A.add)
-        ts(half("INV", par), lists(par), 0.5, A.is_lt, 4096.0, A.mult)
+        act(half("INV", par), lists(par), -4096.0, c("LNB"), F.Relu)
 
     for par in (0, 1):
         ts(lists(par), c("GLI", par, 320, 2), 1.0, A.add)
-        ts(half("VAL", par), lists(par), 0.5, A.is_ge)
+        act(half("VAL", par), lists(par), 1.0, 0.0, F.Sign)
     mms([(c("P7", 0, 320), c("B1"), c("VAL"), True, True)])
     ts(c("NT"), c("P7", 0, 320), 4.0, A.mult, 4.0, A.add)
     act(c("NS"), c("P7", 0, 320))
@@ -340,20 +344,14 @@ def rank_program(g, core, T, topo):
         tt(c("KL"), c("P7", 0, 320), c("CK", 320 * q, 320 * q + 320), A.add)
         v, o = c("T1"), c("KL")
         vec(lambda: g.vector.transpose(ap(v), ap(o)), v, [o], 320)
-        for a, n, b in (("T1", 320, "R1"), ("R1", 160, "R2"), ("R2", 80, "R3"), ("R3", 40, "R4")):
-            tt(c(b), c(a, 0, n, 2), c(a, 1, n, 2), A.max)
-        mms([(c("P2", 64 + w, 84, 2), c("EH", 128 * (2 * h + w), 128 * (2 * h + w) + 128), c("R4", h, 20, 2), h == 0, h == 1)
+        scan(c("R1"), c("FL"), c("T1"), A.mult, A.max)
+        mms([(c("P2", 64 + w, 84, 2), c("EH", 128 * (2 * h + w), 128 * (2 * h + w) + 128), c("R1", 16 * h + 15, 320, 32), h == 0, h == 1)
              for w in (0, 1) for h in (0, 1)])
-        ts(c("KB", 20 * q, 20 * q + 20), c("P2", 64, 84), 0.0, A.max)
+        cp(c("KB", 20 * q, 20 * q + 20), c("P2", 64, 84))
 
     NHP, NLP = c("P4", 192, 512), c("P2", 192, 512)
-    ts(c("NG"), c("NBI"), 320.0, A.is_ge, 352.0, A.mult)
-    ts(c("NP"), c("NBI"), 1, A.arith_shift_right)
-    tt(c("NG"), c("NG"), c("NP"), A.add)
-    ts(c("NQ"), c("NBI"), 1, A.bitwise_and)
-    ts(c("NPF"), c("NQ"), 160.0, A.mult)
     for par in (0, 1):
-        tt(half("NCF", par), c("NG", par, 320, 2), c("NPF", par, 320, 2), A.add)
+        cp(half("NCF", par), c("NBI", par, 320, 2))
     act(c("NH"), c("NCF"))
     act(NHP, c("NH"))
     tt(NLP, c("NCF"), NHP, A.subtract)
@@ -384,8 +382,8 @@ def rank_program(g, core, T, topo):
     ts(c("EVW", 0, 128, 2), c("B1", 0, 128, 2), 1.0 / 512, A.mult)
     ts(c("ODW", 1, 128, 2), c("B1", 1, 128, 2), 1.0 / 512, A.mult)
     ts(c("FL"), c("KC"), 0.5, A.is_ge)
-    ts(c("K15"), c("KC"), -1.0, A.mult, 15.0, A.add)
-    ts(c("K10"), c("KC"), 1024.0, A.mult)
+    ts(c("K15"), c("KC", 0, 160), -1.0, A.mult, 15.0, A.add)
+    ts(c("K10"), c("KC", 0, 160), 1024.0, A.mult)
     ts(c("CJ"), c("CJ"), c("LN"), A.add)
     ts(c("CJ"), c("CJ"), 3277.0, A.mult)
     ts(c("CJ"), c("CJ"), 16, A.arith_shift_right)
@@ -405,7 +403,7 @@ def rank_program(g, core, T, topo):
         tt(c("EQ"), at(c("GL1", 168 * par, 168 * par + 168), c("EU")), c("MA1"), A.is_equal)
         tt(c("W3", 0, 320), c("EQ"), NHP, A.mult)
         tt(c("W3", 320, 640), c("EQ"), NLP, A.mult)
-        ts(c("W3", 640, 960), c("EQ"), c("LK1"), A.mult)
+        act(c("W3", 640, 960), c("EQ"), c("LK1"))
         gather_lanes(c("P6", 0, 60), "W3", 0, 60)
         ts(c("X1"), c("EI"), 4.0, A.mult, 2.0 * par + 1.0, A.add)
         tt(c("X2"), c("AC"), c("X1"), A.mult)
@@ -419,14 +417,15 @@ def rank_program(g, core, T, topo):
         ts(c("X4"), c("E4"), 16.0, A.mult)
         tt(c("X7"), c("X7"), c("X4"), A.add)
         ts(c("A3"), c("P6", 0, 60), 1.0 / 64, A.mult)
-        tt(c("CI"), c("A3", 0, 20), c("A3", 20, 40), A.add)
-        cp(c("OU"), c("CI"))
-        ts(c("X3"), c("CI"), 512.0, A.is_ge, 704.0, A.mult)
-        ts(c("E2"), c("CI"), 511, A.bitwise_and)
-        ts(c("X5"), c("E2"), 160.0, A.is_ge, 319.0, A.mult)
-        tt(c("X3"), c("X3"), c("X5"), A.add)
-        ts(c("X5"), c("CI"), 2.0, A.mult)
-        tt(c("OF"), c("X5"), c("X3"), A.subtract)
+        tt(c("OF"), c("A3", 0, 20), c("A3", 20, 40), A.add)
+        cp(c("CI"), c("OF"))
+        ts(c("X3"), c("OF"), 320.0, A.is_ge, 352.0, A.mult)
+        ts(c("E2"), c("CI"), 1, A.bitwise_and)
+        ts(c("CS1"), c("CI"), 1, A.arith_shift_right)
+        ts(c("X5"), c("E2"), 160.0, A.mult)
+        tt(c("X8"), c("X3"), c("CS1"), A.add)
+        tt(c("X8"), c("X8"), c("X5"), A.add)
+        cp(c("OU"), c("X8"))
         tt(c("Y2"), c("OF"), c("A21"), A.mult)
         ts(c("MM2", 20, 40), c("OF"), 2.0, A.mult, 37.0, A.add)
         ts(c("YS"), c("Y2"), 4, A.arith_shift_right)
@@ -499,8 +498,8 @@ def rank_program(g, core, T, topo):
         for j in range(4):
             tt(c("X", 320 * j, 320 * j + 320), at(c("RW", 0, 4096), c("IXU", 20 * j, 20 * j + 20)), c("ZE"), A.max)
         gather_lanes(c("P3", 0, 80), "X", 0, 80)
-        for hf in (0, 80):
-            act(c("DG", 16 * hf, 16 * hf + 1280), at(c(dw, 0, 320), c("AOU", po + hf, po + hf + 80)))
+        for hf in (0, 40, 80, 120):
+            act(c("DG", 16 * hf, 16 * hf + 640), at(c(dw, 0, 320), c("AOU", po + hf, po + hf + 40)))
         mms([(c("P4", 0, 160), SS(k), c("DG", k, 2560, 16), k == 0, k == 15) for k in range(16)])
         tt(c("P0", 320, 480), half("M2A", par), c("P0", po, po + 160), A.mult)
         tt(c("UC"), half("BU", par), c("P0", 320, 480), A.add)
@@ -531,19 +530,28 @@ def rank_program(g, core, T, topo):
         act(c("RN"), at(c("RW", 0, 4096), c("IXN", 0, 20)))
         for hf in (0, 80):
             act(c(gw, 16 * hf, 16 * hf + 1280), at(c("RW"), c("UI", hf, hf + 80)))
-        scan(c("S1"), c("FL"), c("P5", 0, 160), A.mult, A.max)
+        scan(c("S1"), c("FL", 0, 160), c("P5", 0, 160), A.mult, A.max)
         tt(c("QE"), c("S1"), c("P5", 0, 160), A.is_equal)
         tt(c("QY"), c("QE"), c("P7", 320, 480), A.mult)
-        scan(c("S2"), c("FL"), c("QY"), A.mult, A.max)
+        scan(c("S2"), c("FL", 0, 160), c("QY"), A.mult, A.max)
         tt(c("inj"), c("S1", 15, 160, 16), c("thr"), A.is_gt)
         cp(c("y"), c("S2", 15, 160, 16))
         ts(c("code"), c("y"), 1023, A.bitwise_and)
-        ts(c("gh"), c("code"), 512.0, A.is_ge)
+        ts(c("gh"), c("code"), 320.0, A.is_ge)
+        if t == 1:
+            names(0)
+            keys(0, 0)
+            places(0)
+            sizes_at_entries(0)
+            elect(0)
         tt(c("xb"), c("inj"), c("gh"), A.mult)
         mms([(c("P5", 192, 202), c("B1"), c("xb"), True, True), (c("P5", 208, 218), c("NTRI"), c("xb"), True, True)])
-        ts(c("wi"), c("code"), 15, A.bitwise_and)
+        ts(c("wi"), c("code"), 1, A.arith_shift_right, 15, A.bitwise_and)
+        ts(c("pb"), c("code"), 1, A.bitwise_and)
+        ts(c("p10"), c("pb"), 10.0, A.mult)
         ts(c("w"), c("wi"), 1.0, A.add)
-        ts(c("hh"), c("code"), 4, A.arith_shift_right)
+        ts(c("h5"), c("code"), 5, A.arith_shift_right)
+        tt(c("hh"), c("h5"), c("p10"), A.add)
         for x in range(10):
             ts(c("LH", 128 * x, 128 * x + 128), c("BLC"), c("w", x, x + 1), A.is_equal)
         tt(c("xh"), c("xb"), c("hh"), A.mult)
@@ -553,8 +561,8 @@ def rank_program(g, core, T, topo):
         tt(c("HF", 0, 10), c("prf"), c("xh"), A.mult)
         tt(c("RH"), at(c("HF"), c("COFF", 0, 13)), c("IOT"), A.is_equal)
         mms([(c("P6", 64, 84), c("LH", 128 * x, 128 * x + 128), c("RH", 20 * x, 20 * x + 20), x == 0, x == 9) for x in range(10)])
-        cp(c("CS%d" % t), c("P6", 64, 84))
-        send(rank + 1, rank - 1, c("CL%d" % t), c("CS%d" % t), "ac%d" % t)
+        cp(c("CN%d" % t), c("P6", 64, 84))
+        send(rank + 1, rank - 1, c("CL%d" % t), c("CN%d" % t), "ac%d" % t)
         cp(at(c(gw), c("PU", 0, 20)), c("RN"))
         scan(c("GS"), c("FLB"), c(gw, 0, 2560), A.mult, A.max)
         tt(c("ZA"), c(zw, 0, 160), c("GS", 15, 2560, 16), A.add)
@@ -562,18 +570,16 @@ def rank_program(g, core, T, topo):
         cp(c("ZS%d" % t), c("ZB"))
         send(rank + 1 + t, rank - 1 - t, c("Z%d" % (t + 1), 0, 160), c("ZS%d" % t), "az%d" % (t + 1))
         l1, ns, last = lists(par), half("NS", par), t == RO - 1
-        ts(c("NK"), ns, c("LN"), A.is_equal)
+        act(c("NKA"), ns, 1.0, c("LNN"), F.Abs)
+        act(c("NK"), c("NKA"), -1.0, c("ON1"), F.Relu)
         act(c("JB", 160, 320), ns)
         gather_lanes(c("P2", 144, 154), "JB", 160, 10)
         ts(c("n15"), c("P2", 144, 154), 15.5 * 1024, A.is_le)
         ts(c("ng"), c("gh"), 0.5, A.is_lt)
         tt(c("cc"), c("inj"), c("n15"), A.mult)
         tt(c("cd"), c("cc"), c("ng"), A.mult)
-        ts(c("c5"), c("code"), 511, A.bitwise_and)
-        ts(c("pu"), c("c5"), 160.0, A.is_ge)
-        ts(c("k1"), c("pu"), -319.0, A.mult, 1.0, A.add)
-        ts(c("oo"), c("c5"), 2.0, A.mult)
-        tt(c("op"), c("oo"), c("k1"), A.add)
+        ts(c("op"), c("code"), 1.0, A.add)
+        ts(c("o2"), c("code"), 1, A.arith_shift_right)
         tt(c("xi"), c("op"), c("cd"), A.mult)
         ts(c("jh"), c("xi"), 496, A.bitwise_and)
         ts(c("jl"), c("xi"), 15, A.bitwise_and)
@@ -583,27 +589,28 @@ def rank_program(g, core, T, topo):
         tt(c("JQ"), l1, c("P1", 0, 160), A.is_equal)
         mms([(c("P3", 128, 288), c("B1"), c("JQ"), True, True)])
         if not last:
-            cp(c("CU"), c("c5"))
-            cp(c("JB", 0, 160), at(c("NT"), c("CU")))
+            ts(c("p16"), c("pb"), 160.0, A.mult)
+            tt(c("k1"), c("p16"), c("o2"), A.add)
+            ts(c("k1"), c("k1"), 319.0, A.min)
+            cp(c("CU"), c("k1"))
+            act(c("JB", 0, 160), at(c("NT"), c("CU")))
         ts(c("JA"), c("P3", 128, 288), 0.5, A.is_lt)
         jv, jw = c("P1", 160, 320), c("P1", 320, 480)
         tt(jv, c("JA"), c("P1", 0, 160), A.mult)
         if not last:
-            ts(c("JB", 320, 480), jv, 0.5, A.is_ge)
+            act(c("JB", 320, 480), jv, 1.0, 0.0, F.Sign)
             gather_lanes(c("P2", 96, 126), "JB", 0, 30)
         tt(jw, c("NK"), jv, A.mult)
         tt(l1, l1, jw, A.add)
-        ts(c("YL", par, 320, 2), l1, -1.0, A.add)
+        act(c("YL", par, 320, 2), l1, 1.0, -1.0)
         if not last:
             if t == 0:
                 tt(ns, ns, c("JB", 320, 480), A.add)
             act(c("J3"), c("P2", 96, 126))
             ts(c("k2"), c("J3", 10, 20), -0.25, A.mult, 3680.0, A.add)
-            ts(c("k3"), c("pu"), -160.0, A.mult)
-            tt(c("k5"), c("k3"), c("c5"), A.add)
-            ts(c("k4"), c("pu"), float(1 - par), A.is_equal, 1.0 / 1024, A.mult)
+            ts(c("k4"), c("pb"), float(1 - par), A.is_equal, 1.0 / 1024, A.mult)
             tt(c("k6"), c("k2"), c("J3", 0, 10), A.add)
-            tt(c("k7"), c("k6"), c("k5"), A.add)
+            tt(c("k7"), c("k6"), c("o2"), A.add)
             tt(c("k8"), c("k4"), c("J3", 20, 30), A.mult)
             tt(c("k9"), c("k7"), c("k8"), A.mult)
             kb = c("KB", 20 * (1 - par) + 10 * par, 20 * (1 - par) + 10 * par + 10)
@@ -621,23 +628,17 @@ def rank_program(g, core, T, topo):
             if t == 0:
                 cur[0] = 0
                 ts(c("NT", 0, 160), c("NS", 0, 160), 4.0, A.mult, 4.0, A.add)
-                names(0)
-                keys(0, 0)
-                places(0)
-                sizes_at_entries(0)
-                elect(0)
 
     cur[0] = (RO - 1) & 1
     pn = c("PN")
     dma("Y", T.yl[:, :], ap(c("YL")), "d_yl", [c("YL")], [], 2.2)
     cur[0] = RO & 1
     tt(c("SI"), pn, c("CL%d" % (RO - 1)), A.add)
-    cp(c("SO"), c("SI"))
+    ts(c("PJM", 0, 20), c("SI"), 15, A.bitwise_and)
+    cp(c("SO"), c("PJM", 0, 20))
     spread("P0", c("SO"), 20)
-    cp(c("YDI"), c("P0", 0, 320))
-    ts(c("YDJ"), c("YDI"), 15, A.bitwise_and)
     for par in (0, 1):
-        cp(c("YD", par, 320, 2), half("YDJ", par))
+        cp(c("YD", par, 320, 2), c("P0", 160 * par, 160 * par + 160))
     dma("S", T.yd[:, :], T["YD"][0:128:16, :], "d_yd", [c("YD")], [], 2.0)
     dma("Y", T.yz[:, :], ap(c("Z%d" % RO, 0, 160)), "d_yz", [c("Z%d" % RO, 0, 160)], [], 2.2)
 
@@ -660,11 +661,21 @@ def rank_program(g, core, T, topo):
     while len(order) < len(ops):
         best = None
         for q in pool:
-            for k in pool[q]:
-                s = ready[k] if q == "A" else max(free[q], ready[k])
-                key = (s, -prio[k], k)
-                if best is None or key < best[0]:
-                    best = (key, q, k)
+            if not pool[q]:
+                continue
+            start = lambda k: ready[k] if q == "A" else max(free[q], ready[k])
+            k = min(pool[q], key=lambda k: (start(k), -prio[k], k))
+            for _ in range(6):
+                s = start(k)
+                up = [j for j in pool[q] if prio[j] > prio[k] and s < start(j) < s + 0.6 * ops[k]["cost"]]
+                if q == "A" or not up:
+                    break
+                j = max(up, key=lambda j: (prio[j], -j))
+                fit = [i for i in pool[q] if i != k and start(i) + ops[i]["cost"] <= start(j)]
+                k = max(fit, key=lambda i: (prio[i], -i)) if fit else j
+            key = (start(k), -prio[k], k)
+            if best is None or key < best[0]:
+                best = (key, q, k)
         (s, _, k), q, _ = best
         pool[q].remove(k)
         d = ops[k]

from concourse.mybir import AluOpType as A, AxisListType, ActivationFunctionType as F

N, RO, CAP = 8, 3, 28
BIG = 524288.0

SCRATCH = {}
VIEW = {}
_TYPES = {"f": "float32", "i": "int32", "b": "bfloat16", "u": "uint16"}
_fill = {}


def _own(name, width, kind):
    SCRATCH[name] = ("sbuf", [128, width], _TYPES[kind])
    VIEW[name] = (name, 0, width)


def _put(name, width, kind):
    tag = "ar" + kind
    o = _fill.get(tag, 0)
    VIEW[name] = (tag, o, width)
    _fill[tag] = o + (width + 15) // 16 * 16
    SCRATCH[tag] = ("sbuf", [128, _fill[tag]], _TYPES[kind])


for _n, _w in (("BLP", 128), ("CM1", 128), ("B1", 128), ("BLC", 128), ("ALL1", 128), ("MIN1", 128), ("NTRI", 128), ("EVW", 128), ("ODW", 128), ("ID", 128),
               ("VAL", 320), ("NT", 320), ("NH", 320), ("R8", 640), ("SEL8", 128), ("THL", 320), ("SEL0", 128), ("K15", 160), ("K10", 160)):
    _put(_n, _w, "b")
for _n, _w in (("ONF", 128), ("LN", 1), ("LN2", 1), ("LNB", 1), ("LNC", 1), ("LNN", 1), ("ON1", 1), ("LK1", 1), ("LC0", 1), ("LC1", 1),
               ("AC", 20), ("DMP", 20), ("A21", 20), ("CM40", 40),
               ("MA1", 320), ("M1V", 320), ("V21", 320), ("KC", 320), ("FL", 320), ("IOT", 208),
               ("AO", 320), ("HA", 320), ("M2A", 320), ("BU", 320), ("INV", 320), ("CT", 320), ("CK", 640), ("NS", 320), ("KB", 40),
               ("NCF", 320), ("V8F", 160), ("TH2", 20), ("th64", 10), ("YL", 320), ("EMP", 320)):
    _put(_n, _w, "f")
for _n, _w in (("LI", 1), ("TI", 20), ("TJ", 20), ("CJ", 14), ("NA", 320), ("PB", 320), ("BUI", 320)):
    _put(_n, _w, "i")
for _n, _w in (("AOU", 320), ("COFF", 14)):
    _put(_n, _w, "u")
LOCAL = set()
for _k, _l in (("f", (("T1", 320), ("KL", 320), ("R1", 320), ("A3", 60), ("X1", 20), ("X3", 20), ("X4", 20), ("X5", 20),
                      ("X6", 20), ("X7", 20), ("X8", 20), ("OF", 20), ("NM", 20), ("DN", 20), ("PX", 40), ("MM2", 40), ("BB2", 40), ("JC", 80), ("J2", 80), ("TP", 100),
                      ("U", 40), ("B40", 40), ("PQ", 40), ("UC", 160), ("S1", 160), ("QE", 160), ("QY", 160), ("S2", 160), ("HF", 16),
                      ("CC", 2), ("JA", 160), ("J3", 30), ("NKA", 160), ("p10", 10), ("p16", 10),
                      ("thr", 10), ("gh", 10), ("xh", 10), ("cs", 10), ("pre", 10), ("prf", 10), ("w", 10), ("cd", 10), ("op", 10),
                      ("ng", 10), ("n15", 10), ("cc", 10), ("k1", 10), ("k2", 10), ("k4", 10), ("k6", 10), ("k7", 10), ("k8", 10), ("k9", 10))),
                ("i", (("E1", 20), ("EI", 20), ("E2", 20), ("E3", 20), ("E4", 20), ("X2", 20), ("XS", 20), ("Y2", 20), ("YS", 20), ("CI", 20), ("CS1", 20), ("SI", 20),
                       ("PJ", 80), ("PJM", 80), ("SGI", 20), ("SGJ", 20), ("T6", 100), ("IX", 100), ("KI", 80), ("KJ", 40), ("KK", 20), ("PN", 20), ("IN", 40), ("IM", 40),
                       ("UE", 160), ("UF", 160), ("UG", 160), ("y", 10), ("code", 10), ("wi", 10), ("pb", 10), ("h5", 10), ("o2", 10), ("hh", 10),
                       ("xi", 10), ("jh", 10), ("jl", 10), ("CCI", 1), ("CCJ", 1), ("ZA", 160), ("ZB", 160))),
                ("b", (("EQ", 320), ("W3", 960), ("OEB", 320), ("SO", 20), ("SGH", 20), ("QD", 640), ("ZE", 320), ("X", 1280), ("XO", 320), ("NXO", 320),
                       ("XN", 320), ("RN", 320), ("DG", 2560), ("RH", 208), ("LH", 1280), ("JHL", 20), ("JQ", 160), ("NK", 160), ("JB", 480),
                       ("inj", 10), ("xb", 10))),
                ("u", (("EU", 20), ("OU", 20), ("PU", 40), ("IXU", 100), ("IXN", 40), ("UI", 160), ("CU", 10)))):
    for _n, _w in _l:
        LOCAL.add(_n)
        for _i in (0, 1):
            _put(_n + "#%d" % _i, _w, _k)
for _i in (0, 1):
    _own("DWa%d" % _i, 832, "b")
    _own("Ga%d" % _i, 2880, "b")
    _own("OWa%d" % _i, 2880, "b")
for _n, _w, _k in (("GLI", 320, "i"), ("NBI", 320, "i"), ("V8I", 640, "i"), ("RW", 4112, "b"), ("SS", 2048, "b"), ("EX", 2048, "b"), ("EH", 512, "f"),
                   ("FLB", 2560, "b"), ("SG", 5120, "b"), ("GS", 2560, "b"), ("GL1", 336, "f"), ("YD", 320, "f"), ("GDI", 20, "b")):
    _own(_n, _w, _k)
for _t in range(RO):
    _own("DX%d" % _t, 2880, "b")
    for _n in ("CN", "CL", "GD", "GH"):
        _own("%s%d" % (_n, _t), 20, "b")
    _own("ZS%d" % _t, 160, "b")
for _t in range(RO + 1):
    _own("Z%d" % _t, 176, "b")
for _t in range(8):
    SCRATCH["P%d" % _t] = ("psum", [128, 512], "float32")
    VIEW["P%d" % _t] = ("P%d" % _t, 0, 512)
SEMAPHORES = ["sV", "sS", "sT", "sG", "loc", "ac0", "ac1", "ac2", "ag0", "ag1", "ag2", "az1", "az2", "az3",
              "d_gl", "d_val", "d_th", "d_nb", "d_zl", "d_rec", "d_x1", "d_x2", "d_o0", "d_o1", "d_yl", "d_yd", "d_yz"]


def rank_program(g, core, T, topo):
    rank = T.rank_of(core)
    if rank is None:
        return
    cores = list(T.cores)
    queue = {"V": g.vector, "S": g.scalar, "T": g.tensor, "G": g, "Y": g.sync}
    cur = [0]
    ops = []
    acc = {}

    def c(name, lo=0, hi=None, step=1, np=128):
        buf, o, w = VIEW[name + "#%d" % cur[0] if name in LOCAL else name]
        return (buf, o + lo, o + (w if hi is None else hi), step, np)

    def meet(a, lo, hi, step):
        if a[1] <= lo or hi <= a[0]:
            return False
        return not (a[2] == step and step > 1 and a[0] % step != lo % step)

    def node(q, calls, outs, ins, cost, lat=0.0, **kw):
        r, w = [], []
        for v in ins:
            if isinstance(v, tuple):
                r += [v[1], v[2]] if v[0] == "@" else [v]
        for v in outs:
            if v[0] == "@":
                w.append(v[1])
                r.append(v[2])
            else:
                w.append(v)
        k, preds = len(ops), {}
        for kind, views in ((0, r), (1, w)):
            for (name, lo, hi, step, np) in views:
                psum = SCRATCH[name][0] == "psum"
                for a in acc.get(name, []):
                    oq = ops[a[4]]["q"]
                    if psum and oq != q:
                        preds[a[4]] = True
                        continue
                    if not meet(a, lo, hi, step) or (a[3] == 0 and kind == 0):
                        continue
                    soft = oq == q and q == "T"
                    preds[a[4]] = preds.get(a[4], False) or not soft
        for (name, lo, hi, step, np) in w:
            acc[name] = [a for a in acc.get(name, []) if not (lo <= a[0] and a[1] <= hi and step == 1 and np == 128)]
            acc[name].append([lo, hi, step, 1, k])
        for (name, lo, hi, step, np) in r:
            acc.setdefault(name, []).append([lo, hi, step, 0, k])
        d = {"q": q, "calls": calls, "preds": preds, "cost": cost, "lat": lat}
        d.update(kw)
        ops.append(d)
        return k

    def ap(v):
        name, lo, hi, step, np = v
        return T[name][0:np, lo:hi:step] if np != 128 else T[name][:, lo:hi:step]

    def opnd(v):
        if isinstance(v, tuple):
            return ap(v[1]).indirect(ap(v[2])) if v[0] == "@" else ap(v)
        return v

    def at(win, off):
        return ("@", win, off)

    def width(v):
        return 16 * (v[2][2] - v[2][1]) if v[0] == "@" else -(-(v[2] - v[1]) // v[3])

    def size2(v):
        return SCRATCH[(v[1] if v[0] == "@" else v)[0]][2] in ("bfloat16", "uint16")

    def cyc(out, ins, two=False):
        n = width(out)
        if out[0] == "@":
            return 60 + 3.0 * n
        if any(v[0] == "@" for v in ins):
            return 60 + 1.56 * n
        if two:
            return n * (1 if any(SCRATCH[v[0]][0] == "psum" for v in ins) else 2)
        return n * (0.5 if all(size2(v) for v in [out] + ins) else 1)

    def vec(call, out, ins, cy):
        node("V", [call], [out], ins, max(64.0, cy) * 0.00104)

    def tt(out, a, b, op):
        vec(lambda: g.vector.tensor_tensor(opnd(out), opnd(a), opnd(b), op), out, [a, b], cyc(out, [a, b], True))

    def ts(out, a, s1, op0, s2=None, op1=None):
        if op1 is None:
            vec(lambda: g.vector.tensor_scalar(opnd(out), opnd(a), opnd(s1), None, op0), out, [a, s1], cyc(out, [a]))
        else:
            vec(lambda: g.vector.tensor_scalar(opnd(out), opnd(a), opnd(s1), opnd(s2), op0, op1), out, [a, s1, s2], cyc(out, [a]))

    def cp(out, a):
        vec(lambda: g.vector.tensor_copy(opnd(out), opnd(a)), out, [a], cyc(out, [a]))

    def act(out, a, scale=1.0, bias=0.0, func=F.Copy):
        n = width(out)
        cost = (78 + 1.56 * n if a[0] == "@" else 60 + n) * 0.00104
        node("S", [lambda: g.scalar.activation(opnd(out), opnd(a), func, bias=opnd(bias), scale=opnd(scale))], [out], [a, bias, scale], cost)

    def scan(out, d0, d1, op0, op1):
        vec(lambda: g.vector.tensor_tensor_scan(ap(out), ap(d0), ap(d1), 0.0, op0, op1), out, [d0, d1], cyc(out, [d0, d1]))

    def mms(lst):
        calls = [lambda o=o, l=l, r=r, s=s, e=e: g.tensor.matmul(ap(o), ap(l), ap(r), s, e) for o, l, r, s, e in lst]
        cost = sum(max(64, width(r)) * (1 if size2(r) else 4) for o, l, r, s, e in lst) * 0.0006
        node("T", calls, [x[0] for x in lst], [x[1] for x in lst] + [x[2] for x in lst], cost)

    def gps(call, out, ins, base):
        node("G", [call], [out], ins, base + width(out) * 0.002)

    def iota(v, pattern, base, cm):
        if SCRATCH[v[0]][2] != "int32":
            gps(lambda: g.iota(ap(v), pattern, base, cm, allow_small_or_imprecise_dtypes=True), v, [], 0.14)
        else:
            gps(lambda: g.iota(ap(v), pattern, base, cm), v, [], 0.14)

    def const(v, x):
        for lo in range(v[1], v[2], 720 * v[3]):
            p = (v[0], lo, min(v[2], lo + 720 * v[3]), v[3], v[4])
            iota(p, [[0, width(p)]], x, 0)

    def select(out, a, pattern, op, base, cm):
        gps(lambda: g.affine_select(ap(out), ap(a), pattern, op, 0.0, base, cm), out, [a], 0.18)

    def dma(q, out_ap, in_ap, sem, reads, writes, lat):
        node(q, [lambda: queue[q].dma_start(out_ap, in_ap)], writes, reads, 0.1, lat, sem=sem)

    def send(dst_rank, src_rank, out_v, in_v, sem):
        dst = cores[dst_rank % N]
        m = topo.mask(core, dst)
        rid, pid, _ = topo.addr(dst)
        k = node("G", [lambda: g.remote_dma(ap(out_v), ap(in_v), T.sem[sem], T.sem.loc, pid, rid, m)], [], [in_v], 0.3,
                 sent=len(topo.engines(core, dst)))
        n = len(topo.engines(cores[src_rank % N], core))
        ops.append({"q": "A", "calls": [], "preds": {k: False}, "cost": 0.0, "lat": 1.8, "sem": sem, "amount": n})
        acc[out_v[0]] = [a for a in acc.get(out_v[0], []) if not meet(a, out_v[1], out_v[2], 1)]
        acc[out_v[0]].append([out_v[1], out_v[2], 1, 1, len(ops) - 1])

    SS = lambda b: c("SS", 128 * b, 128 * b + 128)
    EX = lambda b: c("EX", 128 * b, 128 * b + 128)

    def gather_lanes(out, src, lo, n):
        mms([(out, SS(b), c(src, lo + b, lo + 16 * n, 16), b == 0, b == 15) for b in range(16)])

    def spread(bank, src, n):
        mms([(c(bank, b, 16 * n, 16), EX(b), src, True, True) for b in range(16)])

    def half(n, par, d=0):
        return c(n, d + 160 * par, d + 160 * par + 160)

    def lists(par):
        return c("GL1", 168 * par, 168 * par + 160)

    dma("Y", ap(c("GLI")), T.gl[:, :], "d_gl", [], [c("GLI")], 2.2)
    dma("S", ap(c("V8I", 0, 320, 1, 8)), T.val[:, :], "d_val", [], [c("V8I", 0, 320)], 1.9)
    dma("Y", ap(c("NBI")), T.nb[:, :], "d_nb", [], [c("NBI")], 2.4)
    dma("S", ap(c("V8I", 320, 480, 1, 8)), T.th[:, :], "d_th", [], [c("V8I", 320, 480)], 1.9)
    dma("Y", ap(c("Z0", 0, 160)), T.zl[:, :], "d_zl", [], [c("Z0", 0, 160)], 2.5)
    dma("Y", ap(c("RW", 0, 4096)), T.rec[:, :], "d_rec", [], [c("RW", 0, 4096)], 6.0)

    ingroup = [[-16, 8], [0, 16]]
    const(c("ALL1"), 1)
    select(c("BLP"), c("ALL1"), ingroup, A.is_ge, 0, 1)
    select(c("B1"), c("BLP"), [[16, 8], [0, 16]], A.is_ge, 15, -1)
    iota(c("CM1"), [[0, 8], [1, 16]], 1, 0)
    iota(c("LI"), [[0, 1]], 0, 1)
    iota(c("SEL0", 0, 128, 1, 8), [[-1, 8], [0, 16]], 0, 1)
    const(c("ONF"), 1)
    for h in (0, 1):
        for w in (0, 1):
            e = 128 * (2 * h + w)
            select(c("EH", e, e + 128), c("ONF"), [[-32, 4], [1000, 2], [-1, 16]], A.is_equal, -1000 * h - 16 * w, 1)
    for b in range(16):
        select(EX(b), c("ALL1"), ingroup, A.is_equal, -b, 1)
    iota(c("TI"), [[1, 2], [32, 10]], 0, 0)
    iota(c("TJ"), [[160, 2], [16, 10]], 2560, 0)
    iota(c("MA1"), [[1, 2], [2, 160]], 1, 0)
    iota(c("M1V"), [[2, 2], [4, 160]], 613, 0)
    iota(c("V21"), [[2, 2], [4, 160]], 1, 0)
    for i in (0, 1):
        const(c("DWa%d" % i, 320, 512), 0)
    for t in range(RO + 1):
        const(c("Z%d" % t, 160, 176), 0)
    iota(c("KC"), [[0, 20], [1, 16]], 0, 0)
    const(c("RW", 4096, 4112), 0)
    zero = c("DX0")
    vec(lambda: g.vector.memset(ap(zero), 0.0), zero, [], 1440)
    const(c("MIN1"), -1)
    select(c("ID"), c("ALL1"), [[-1, 128]], A.is_equal, 0, 1)
    select(c("NTRI"), c("MIN1"), [[-16, 8], [-1, 16]], A.is_gt, 0, 1)
    select(c("NTRI"), c("NTRI"), [[16, 8], [0, 16]], A.is_ge, 15, -1)
    const(c("FLB"), 1)
    const(c("FLB", 0, 2560, 16), 0)
    iota(c("IOT", 0, 200), [[0, 10], [1, 20]], 10, 0)
    const(c("IOT", 200, 208), 0)
    iota(c("CJ"), [[16, 14]], 0, 0)
    for i in (1, 0):
        cur[0] = i
        const(c("HF"), 0)
        const(c("JC", 0, 20), 0)
    for n, s in (("OWa0", "d_o0"), ("OWa1", "d_o1"), ("DX1", "d_x1"), ("DX2", "d_x2")):
        dma("Y", ap(c(n)), ap(c("DX0")), s, [c("DX0")], [c(n)], 4.0)
    const(c("GL1", 160, 168), -5)
    const(c("GL1", 328, 336), -5)
    for n in ("EVW", "ODW"):
        const(c(n), 0)

    tt(c("BLC"), c("CM1"), c("B1"), A.mult)
    ts(c("LI"), c("LI"), 15, A.bitwise_and)
    cp(c("LN"), c("LI"))
    ts(c("LN2"), c("LN"), 2.0, A.mult)
    const(c("LNB"), 4096)
    const(c("LNC"), int(BIG))
    const(c("ON1"), 1)
    ts(c("LNN"), c("LN"), -1.0, A.mult)
    ts(c("LK1"), c("LN"), 1.0, A.add)
    ts(c("LC0"), c("LN"), -256.0, A.mult, 3680.0, A.add)
    ts(c("LC1"), c("LC0"), BIG, A.subtract)
    for b in range(16):
        ts(SS(b), c("BLC"), float(b + 1), A.is_equal, 64.0, A.mult)

    def names(par):
        ts(half("NA", par), lists(par), -1.0, A.add)
        ts(half("PB", par), half("NA", par), 1, A.bitwise_and)
        act(half("HA", par), lists(par), 0.5, -0.5)
        ts(half("AO", par), half("PB", par), 159.5, A.mult)
        tt(half("AO", par), half("AO", par), half("HA", par), A.add)
        cp(half("AOU", par), half("AO", par))

    def keys(par, q):
        if q == 0:
            ts(half("CT", par), half("PB", par), -BIG - 0.5, A.mult, c("LC0"), A.add)
            tt(half("CK", par), half("CT", par), half("HA", par), A.add)
        else:
            act(half("EMP", par), lists(par), -BIG, c("LNC"), F.Relu)
            ts(half("CT", par), half("PB", par), BIG - 0.5, A.mult, c("LC1"), A.add)
            tt(half("CT", par), half("CT", par), half("EMP", par), A.subtract)
            tt(half("CK", par, 320), half("CT", par), half("HA", par), A.add)

    def places(par):
        act(half("M2A", par), lists(par), 2.0, 35.0)
        tt(half("BUI", par), half("NA", par), half("V21", par), A.mult)
        ts(half("BUI", par), half("BUI", par), 4, A.arith_shift_right)
        tt(half("BU", par), half("BUI", par), half("NA", par), A.add)
        act(half("INV", par), lists(par), -4096.0, c("LNB"), F.Relu)

    for par in (0, 1):
        ts(lists(par), c("GLI", par, 320, 2), 1.0, A.add)
        act(half("VAL", par), lists(par), 1.0, 0.0, F.Sign)
    mms([(c("P7", 0, 320), c("B1"), c("VAL"), True, True)])
    ts(c("NT"), c("P7", 0, 320), 4.0, A.mult, 4.0, A.add)
    act(c("NS"), c("P7", 0, 320))
    for par in (0, 1):
        names(par)

    def sizes_at_entries(split):
        for lo, hi in ((split, 160), (160, 240), (240, 320)):
            act(c("SG", 16 * lo, 16 * hi), at(c("NT"), c("AOU", lo, hi)))
        if split:
            cp(c("SG", 0, 16 * split), at(c("NT"), c("AOU", 0, split)))
        for o in (0, 160):
            mms([(c("P7", o, o + 160), SS(k), c("SG", 16 * o + k, 16 * o + 2560, 16), k == 0, k == 15) for k in range(16)])

    def elect(q):
        tt(c("KL"), c("P7", 0, 320), c("CK", 320 * q, 320 * q + 320), A.add)
        v, o = c("T1"), c("KL")
        vec(lambda: g.vector.transpose(ap(v), ap(o)), v, [o], 320)
        scan(c("R1"), c("FL"), c("T1"), A.mult, A.max)
        mms([(c("P2", 64 + w, 84, 2), c("EH", 128 * (2 * h + w), 128 * (2 * h + w) + 128), c("R1", 16 * h + 15, 320, 32), h == 0, h == 1)
             for w in (0, 1) for h in (0, 1)])
        cp(c("KB", 20 * q, 20 * q + 20), c("P2", 64, 84))

    NHP, NLP = c("P4", 192, 512), c("P2", 192, 512)
    for par in (0, 1):
        cp(half("NCF", par), c("NBI", par, 320, 2))
    act(c("NH"), c("NCF"))
    act(NHP, c("NH"))
    tt(NLP, c("NCF"), NHP, A.subtract)
    ts(c("SEL8", 0, 128, 1, 8), c("SEL0", 0, 128, 1, 8), 0.0, A.is_equal)
    cp(c("R8", 0, 320, 1, 8), c("V8I", 0, 320, 1, 8))
    ts(c("V8F", 0, 160, 1, 8), c("V8I", 320, 480, 1, 8), 1.0 / 16, A.mult)
    cp(c("R8", 320, 480, 1, 8), c("V8F", 0, 160, 1, 8))
    tt(c("R8", 480, 640, 1, 8), c("V8F", 0, 160, 1, 8), c("R8", 320, 480, 1, 8), A.subtract)
    mms([(c("P0", 0, 320), c("SEL8", 0, 128, 1, 8), c("R8", 0, 320, 1, 8), True, True)])
    mms([(c("P1", 0, 320), c("SEL8", 0, 128, 1, 8), c("R8", 320, 640, 1, 8), True, True)])
    for par in (0, 1):
        act(c("DWa0", 160 * par, 160 * par + 160), c("P0", par, 320, 2), 1.0 / 1024)
    act(c("THL"), c("P1", 0, 320))
    gather_lanes(c("P2", 0, 20), "DWa0", 0, 20)
    cp(c("GDI"), c("P2", 0, 20))
    cp(c("SO"), c("P2", 0, 20))
    cp(c("PJM", 0, 20), c("P2", 0, 20))
    send(rank - 1, rank + 1, c("GH0"), c("GDI"), "ag0")
    gather_lanes(c("P2", 32, 52), "THL", 0, 20)
    act(c("TH2"), c("P2", 32, 52))
    tt(c("th64"), c("TH2", 0, 10), c("TH2", 10, 20), A.add)
    ts(c("thr"), c("th64"), 15.0, A.add)
    ts(c("AC"), c("TI"), c("LN2"), A.add)
    ts(c("DMP"), c("TJ"), c("LN"), A.add)
    ts(c("A21"), c("AC"), 2.0, A.mult, 1.0, A.add)
    ts(c("CM40", 0, 20), c("AC"), 2.0, A.mult, 37.0, A.add)
    ts(c("CM40", 20, 40), c("AC"), 2.0, A.mult, 613.0, A.add)
    ts(c("EVW", 0, 128, 2), c("B1", 0, 128, 2), 1.0 / 512, A.mult)
    ts(c("ODW", 1, 128, 2), c("B1", 1, 128, 2), 1.0 / 512, A.mult)
    ts(c("FL"), c("KC"), 0.5, A.is_ge)
    ts(c("K15"), c("KC", 0, 160), -1.0, A.mult, 15.0, A.add)
    ts(c("K10"), c("KC", 0, 160), 1024.0, A.mult)
    ts(c("CJ"), c("CJ"), c("LN"), A.add)
    ts(c("CJ"), c("CJ"), 3277.0, A.mult)
    ts(c("CJ"), c("CJ"), 16, A.arith_shift_right)
    cp(c("COFF"), c("CJ"))

    sizes_at_entries(60)
    for par in (0, 1):
        keys(par, 0)
    elect(0)

    def prep(t):
        par = t & 1
        cur[0] = par
        ts(c("E1"), c("KB", 20 * par, 20 * par + 20), 160.0, A.add)
        ts(c("EI"), c("E1"), 255, A.bitwise_and)
        cp(c("EU"), c("EI"))
        tt(c("EQ"), at(c("GL1", 168 * par, 168 * par + 168), c("EU")), c("MA1"), A.is_equal)
        tt(c("W3", 0, 320), c("EQ"), NHP, A.mult)
        tt(c("W3", 320, 640), c("EQ"), NLP, A.mult)
        act(c("W3", 640, 960), c("EQ"), c("LK1"))
        gather_lanes(c("P6", 0, 60), "W3", 0, 60)
        ts(c("X1"), c("EI"), 4.0, A.mult, 2.0 * par + 1.0, A.add)
        tt(c("X2"), c("AC"), c("X1"), A.mult)
        ts(c("XS"), c("X2"), 4, A.arith_shift_right)
        ts(c("MM2", 0, 20), c("EI"), 4.0, A.mult, 2.0 * par + 613.0, A.add)
        tt(c("BB2", 0, 20), c("XS"), c("AC"), A.add)
        ts(c("X6"), c("EI"), 16.0, A.mult, -1.0, A.add)
        ts(c("E3"), c("EI"), 15, A.bitwise_and)
        ts(c("E4"), c("EI"), 4, A.arith_shift_right)
        ts(c("X7"), c("E3"), 160.0, A.mult, -1.0, A.add)
        ts(c("X4"), c("E4"), 16.0, A.mult)
        tt(c("X7"), c("X7"), c("X4"), A.add)
        ts(c("A3"), c("P6", 0, 60), 1.0 / 64, A.mult)
        tt(c("OF"), c("A3", 0, 20), c("A3", 20, 40), A.add)
        cp(c("CI"), c("OF"))
        ts(c("X3"), c("OF"), 320.0, A.is_ge, 352.0, A.mult)
        ts(c("E2"), c("CI"), 1, A.bitwise_and)
        ts(c("CS1"), c("CI"), 1, A.arith_shift_right)
        ts(c("X5"), c("E2"), 160.0, A.mult)
        tt(c("X8"), c("X3"), c("CS1"), A.add)
        tt(c("X8"), c("X8"), c("X5"), A.add)
        cp(c("OU"), c("X8"))
        tt(c("Y2"), c("OF"), c("A21"), A.mult)
        ts(c("MM2", 20, 40), c("OF"), 2.0, A.mult, 37.0, A.add)
        ts(c("YS"), c("Y2"), 4, A.arith_shift_right)
        tt(c("BB2", 20, 40), c("YS"), c("OF"), A.add)
        ts(c("NM"), c("A3", 40, 60), 0.5, A.is_lt)
        tt(c("DN"), c("NM"), c("DMP"), A.mult)
        for j in (1, 2, 3):
            act(c("JC", 20 * j, 20 * j + 20), c("NM"), BIG, 16.0 * j)
        for j, x in ((0, "X6"), (20, "X7")):
            tt(c(x), c(x), c("A3", 40, 60), A.add)
            tt(c("PX", j, j + 20), c(x), c("DN"), A.max)
        cp(c("PU"), c("PX"))
        ow = "OWa%d" % par
        mms([(c("P6", 128, 448), c("EVW"), c("W3", 0, 320), True, False), (c("P6", 128, 448), c("ODW"), c("W3", 320, 640), False, True)])
        act(c("OEB"), c("P6", 128, 448))
        cp(at(c(ow), c("PU", 20, 40)), c("OEB"))
        mms([(c("P7", 320, 480), SS(b), c(ow, 160 * b, 160 * b + 160), b == 0, False) for b in range(16)]
            + [(c("P7", 320, 480), c("ID"), c("K10"), False, True)])
        cur[0] = 1 - par

    prep(0)
    for par in (0, 1):
        keys(par, 1)
    elect(1)
    cur[0] = 0
    places(0)
    places(1)

    for t in range(RO):
        par = t & 1
        po = 160 * par
        cur[0] = par
        zw = "Z%d" % t
        dw = "DWa%d" % par
        if t:
            cur[0] = 1 - par
            pn = c("PN")
            cur[0] = par
            tt(c("SGI"), c("GH%d" % t), c("P6", 64, 84), A.add)
            ts(c("SGJ"), c("SGI"), 15, A.bitwise_and)
            cp(c("SGH"), c("SGJ"))
            spread("P1", c("SGH"), 20)
            act(c(dw, 512, 832), c("P1", 0, 320), 1.0 / 1024)
            tt(c("SI"), pn, c("CL%d" % (t - 1)), A.add)
            ts(c("PJM", 0, 20), c("SI"), 15, A.bitwise_and)
            cp(c("SO"), c("PJM", 0, 20))
            spread("P0", c("SO"), 20)
            ts(c(dw, 0, 320), c("P0", 0, 320), 1.0 / 1024, A.mult)
        else:
            spread("P1", c("GH0"), 20)
            act(c(dw, 512, 832), c("P1", 0, 320), 1.0 / 1024)
            spread("P0", c("SO"), 20)
        cp(c("QD", 0, 320), at(c(dw, po, po + 176), c("EU")))
        act(c("QD", 320, 640), at(c(dw), c("OU")))
        gather_lanes(c("P2", 0, 40), "QD", 0, 40)
        for j in (1, 2, 3):
            ts(c("PJ", 20 * j, 20 * j + 20), c("PJM", 0, 20), float(j), A.add)
        ts(c("PJM", 20, 80), c("PJ", 20, 80), 15, A.bitwise_and)
        for j in range(4):
            tt(c("TP", 20 * j, 20 * j + 20), c("PJM", 20 * j, 20 * j + 20), c("MM2", 0, 20), A.mult)
        tt(c("TP", 80, 100), c("PJM", 0, 20), c("MM2", 20, 40), A.mult)
        tt(c("J2"), c("JC"), c("PJM"), A.add)
        tt(c("U"), c("P2", 0, 40), c("CM40"), A.mult)
        tt(c("B40"), c("BB2"), c("U"), A.add)
        for j in range(5):
            tt(c("T6", 20 * j, 20 * j + 20), c("TP", 20 * j, 20 * j + 20), c("B40", j // 4 * 20, j // 4 * 20 + 20), A.add)
        ts(c("IX"), c("T6"), 4095, A.bitwise_and)
        cp(c("IXU"), c("IX"))
        act(c("ZE"), at(c(zw), c("EU")))
        for j in range(4):
            tt(c("X", 320 * j, 320 * j + 320), at(c("RW", 0, 4096), c("IXU", 20 * j, 20 * j + 20)), c("ZE"), A.max)
        gather_lanes(c("P3", 0, 80), "X", 0, 80)
        for hf in (0, 40, 80, 120):
            act(c("DG", 16 * hf, 16 * hf + 640), at(c(dw, 0, 320), c("AOU", po + hf, po + hf + 40)))
        mms([(c("P4", 0, 160), SS(k), c("DG", k, 2560, 16), k == 0, k == 15) for k in range(16)])
        tt(c("P0", 320, 480), half("M2A", par), c("P0", po, po + 160), A.mult)
        tt(c("UC"), half("BU", par), c("P0", 320, 480), A.add)
        tt(c("P3", 320, 480), half("M1V", par), c("P4", 0, 160), A.mult)
        tt(c("UE"), c("UC"), c("P3", 320, 480), A.add)
        ts(c("UF"), c("UE"), 4095, A.bitwise_and)
        tt(c("UG"), c("UF"), half("INV", par), A.max)
        cp(c("UI"), c("UG"))
        gw = "Ga%d" % par
        tt(c("XO"), at(c("RW", 0, 4096), c("IXU", 80, 100)), c("ZE"), A.max)
        act(c("NXO"), c("XO"), -1.0)
        tt(c("KI"), c("P3", 0, 80), c("J2"), A.add)
        tt(c("KJ"), c("KI", 0, 40), c("KI", 40, 80), A.min)
        tt(c("KK"), c("KJ", 0, 20), c("KJ", 20, 40), A.min)
        ts(c("PN"), c("KK"), 15, A.bitwise_and)
        tt(c("PQ", 20, 40), c("PN"), c("MM2", 20, 40), A.mult)
        tt(c("PQ", 0, 20), c("PN"), c("MM2", 0, 20), A.mult)
        tt(c("IN"), c("PQ"), c("B40"), A.add)
        ts(c("IM"), c("IN"), 4095, A.bitwise_and)
        cp(c("IXN"), c("IM"))
        if t < RO - 1:
            cp(c("GD%d" % t), c("PN"))
            send(rank - 1, rank + 1, c("GH%d" % (t + 1)), c("GD%d" % t), "ag%d" % (t + 1))
        tt(c("XN"), at(c("RW", 0, 4096), c("IXN", 20, 40)), c("ZE"), A.max)
        tt(at(c("DX%d" % t), c("PU", 20, 40)), c("XN"), c("NXO"), A.add)
        mms([(c("P5", 0, 160), SS(b), c("DX%d" % t, 160 * b, 160 * b + 160), b == 0, False) for b in range(16)]
            + [(c("P5", 0, 160), c("ID"), c("K15"), False, True)])
        act(c("RN"), at(c("RW", 0, 4096), c("IXN", 0, 20)))
        for hf in (0, 80):
            act(c(gw, 16 * hf, 16 * hf + 1280), at(c("RW"), c("UI", hf, hf + 80)))
        scan(c("S1"), c("FL", 0, 160), c("P5", 0, 160), A.mult, A.max)
        tt(c("QE"), c("S1"), c("P5", 0, 160), A.is_equal)
        tt(c("QY"), c("QE"), c("P7", 320, 480), A.mult)
        scan(c("S2"), c("FL", 0, 160), c("QY"), A.mult, A.max)
        tt(c("inj"), c("S1", 15, 160, 16), c("thr"), A.is_gt)
        cp(c("y"), c("S2", 15, 160, 16))
        ts(c("code"), c("y"), 1023, A.bitwise_and)
        ts(c("gh"), c("code"), 320.0, A.is_ge)
        if t == 1:
            names(0)
            keys(0, 0)
            places(0)
            sizes_at_entries(0)
            elect(0)
        tt(c("xb"), c("inj"), c("gh"), A.mult)
        mms([(c("P5", 192, 202), c("B1"), c("xb"), True, True), (c("P5", 208, 218), c("NTRI"), c("xb"), True, True)])
        ts(c("wi"), c("code"), 1, A.arith_shift_right, 15, A.bitwise_and)
        ts(c("pb"), c("code"), 1, A.bitwise_and)
        ts(c("p10"), c("pb"), 10.0, A.mult)
        ts(c("w"), c("wi"), 1.0, A.add)
        ts(c("h5"), c("code"), 5, A.arith_shift_right)
        tt(c("hh"), c("h5"), c("p10"), A.add)
        for x in range(10):
            ts(c("LH", 128 * x, 128 * x + 128), c("BLC"), c("w", x, x + 1), A.is_equal)
        tt(c("xh"), c("xb"), c("hh"), A.mult)
        scan(c("cs"), c("ONF", 0, 10), c("P5", 192, 202), A.mult, A.add)
        tt(c("pre"), c("cs"), c("P5", 208, 218), A.add)
        ts(c("prf"), c("pre"), float(CAP), A.is_le)
        tt(c("HF", 0, 10), c("prf"), c("xh"), A.mult)
        tt(c("RH"), at(c("HF"), c("COFF", 0, 13)), c("IOT"), A.is_equal)
        mms([(c("P6", 64, 84), c("LH", 128 * x, 128 * x + 128), c("RH", 20 * x, 20 * x + 20), x == 0, x == 9) for x in range(10)])
        cp(c("CN%d" % t), c("P6", 64, 84))
        send(rank + 1, rank - 1, c("CL%d" % t), c("CN%d" % t), "ac%d" % t)
        cp(at(c(gw), c("PU", 0, 20)), c("RN"))
        scan(c("GS"), c("FLB"), c(gw, 0, 2560), A.mult, A.max)
        tt(c("ZA"), c(zw, 0, 160), c("GS", 15, 2560, 16), A.add)
        ts(c("ZB"), c("ZA"), 1, A.arith_shift_right)
        cp(c("ZS%d" % t), c("ZB"))
        send(rank + 1 + t, rank - 1 - t, c("Z%d" % (t + 1), 0, 160), c("ZS%d" % t), "az%d" % (t + 1))
        l1, ns, last = lists(par), half("NS", par), t == RO - 1
        act(c("NKA"), ns, 1.0, c("LNN"), F.Abs)
        act(c("NK"), c("NKA"), -1.0, c("ON1"), F.Relu)
        act(c("JB", 160, 320), ns)
        gather_lanes(c("P2", 144, 154), "JB", 160, 10)
        ts(c("n15"), c("P2", 144, 154), 15.5 * 1024, A.is_le)
        ts(c("ng"), c("gh"), 0.5, A.is_lt)
        tt(c("cc"), c("inj"), c("n15"), A.mult)
        tt(c("cd"), c("cc"), c("ng"), A.mult)
        ts(c("op"), c("code"), 1.0, A.add)
        ts(c("o2"), c("code"), 1, A.arith_shift_right)
        tt(c("xi"), c("op"), c("cd"), A.mult)
        ts(c("jh"), c("xi"), 496, A.bitwise_and)
        ts(c("jl"), c("xi"), 15, A.bitwise_and)
        cp(c("JHL", 0, 10), c("jh"))
        cp(c("JHL", 10, 20), c("jl"))
        mms([(c("P1", b, 160, 16), EX(b), c("JHL", 10 * h, 10 * h + 10), h == 0, h == 1) for b in range(16) for h in (0, 1)])
        tt(c("JQ"), l1, c("P1", 0, 160), A.is_equal)
        mms([(c("P3", 128, 288), c("B1"), c("JQ"), True, True)])
        if not last:
            ts(c("p16"), c("pb"), 160.0, A.mult)
            tt(c("k1"), c("p16"), c("o2"), A.add)
            ts(c("k1"), c("k1"), 319.0, A.min)
            cp(c("CU"), c("k1"))
            act(c("JB", 0, 160), at(c("NT"), c("CU")))
        ts(c("JA"), c("P3", 128, 288), 0.5, A.is_lt)
        jv, jw = c("P1", 160, 320), c("P1", 320, 480)
        tt(jv, c("JA"), c("P1", 0, 160), A.mult)
        if not last:
            act(c("JB", 320, 480), jv, 1.0, 0.0, F.Sign)
            gather_lanes(c("P2", 96, 126), "JB", 0, 30)
        tt(jw, c("NK"), jv, A.mult)
        tt(l1, l1, jw, A.add)
        act(c("YL", par, 320, 2), l1, 1.0, -1.0)
        if not last:
            if t == 0:
                tt(ns, ns, c("JB", 320, 480), A.add)
            act(c("J3"), c("P2", 96, 126))
            ts(c("k2"), c("J3", 10, 20), -0.25, A.mult, 3680.0, A.add)
            ts(c("k4"), c("pb"), float(1 - par), A.is_equal, 1.0 / 1024, A.mult)
            tt(c("k6"), c("k2"), c("J3", 0, 10), A.add)
            tt(c("k7"), c("k6"), c("o2"), A.add)
            tt(c("k8"), c("k4"), c("J3", 20, 30), A.mult)
            tt(c("k9"), c("k7"), c("k8"), A.mult)
            kb = c("KB", 20 * (1 - par) + 10 * par, 20 * (1 - par) + 10 * par + 10)
            tt(kb, kb, c("k9"), A.max)
            mms([(c("P5", 224, 234), c("ALL1"), c("inj"), True, True)])
            o, i = c("CC", 0, 1), c("P5", 224, 234)
            vec(lambda o=o, i=i: g.vector.tensor_reduce(ap(o), ap(i), AxisListType.X, A.add), o, [i], 10)
            cp(c("CCI"), o)
            ts(c("CCJ"), c("CCI"), 31, A.bitwise_and)
            ts(c("CC", 1, 2), c("CCJ"), 64.0, A.mult, 15.0, A.add)
            inc = c("CC", 1, 2)
            cur[0] = 1 - par
            ts(c("thr"), c("th64"), inc, A.add)
            prep(t + 1)
            if t == 0:
                cur[0] = 0
                ts(c("NT", 0, 160), c("NS", 0, 160), 4.0, A.mult, 4.0, A.add)

    cur[0] = (RO - 1) & 1
    pn = c("PN")
    dma("Y", T.yl[:, :], ap(c("YL")), "d_yl", [c("YL")], [], 2.2)
    cur[0] = RO & 1
    tt(c("SI"), pn, c("CL%d" % (RO - 1)), A.add)
    ts(c("PJM", 0, 20), c("SI"), 15, A.bitwise_and)
    cp(c("SO"), c("PJM", 0, 20))
    spread("P0", c("SO"), 20)
    for par in (0, 1):
        cp(c("YD", par, 320, 2), c("P0", 160 * par, 160 * par + 160))
    dma("S", T.yd[:, :], T["YD"][0:128:16, :], "d_yd", [c("YD")], [], 2.0)
    dma("Y", T.yz[:, :], ap(c("Z%d" % RO, 0, 160)), "d_yz", [c("Z%d" % RO, 0, 160)], [], 2.2)

    succ = [[] for _ in ops]
    for k, d in enumerate(ops):
        for p in d["preds"]:
            succ[p].append(k)
    prio = [0.0] * len(ops)
    for k in range(len(ops) - 1, -1, -1):
        d = ops[k]
        prio[k] = d["cost"] + d["lat"] + max([prio[s] + 0.06 for s in succ[k]], default=0.0)
    left = [len(d["preds"]) for d in ops]
    ready = [0.0] * len(ops)
    pool = {q: [] for q in "VSTGYA"}
    for k, d in enumerate(ops):
        if not left[k]:
            pool[d["q"]].append(k)
    free = {q: 0.0 for q in pool}
    order = []
    while len(order) < len(ops):
        best = None
        for q in pool:
            if not pool[q]:
                continue
            start = lambda k: ready[k] if q == "A" else max(free[q], ready[k])
            k = min(pool[q], key=lambda k: (start(k), -prio[k], k))
            for _ in range(6):
                s = start(k)
                up = [j for j in pool[q] if prio[j] > prio[k] and s < start(j) < s + 0.6 * ops[k]["cost"]]
                if q == "A" or not up:
                    break
                j = max(up, key=lambda j: (prio[j], -j))
                fit = [i for i in pool[q] if i != k and start(i) + ops[i]["cost"] <= start(j)]
                k = max(fit, key=lambda i: (prio[i], -i)) if fit else j
            key = (start(k), -prio[k], k)
            if best is None or key < best[0]:
                best = (key, q, k)
        (s, _, k), q, _ = best
        pool[q].remove(k)
        d = ops[k]
        free[q] = s + d["cost"] + 0.012
        end = s + d["cost"] + d["lat"]
        order.append(k)
        for x in succ[k]:
            gap = 0.06 if ops[x]["preds"][k] else 0.0
            ready[x] = max(ready[x], end + gap)
            left[x] -= 1
            if not left[x]:
                pool[ops[x]["q"]].append(x)

    count = {q: 0 for q in "VSTG"}
    clock = {q: {} for q in "VSTGY"}
    token = [None] * len(ops)
    sent = 0
    for k in order:
        d = ops[k]
        q = d["q"]
        if q == "A":
            token[k] = (d["sem"], d["amount"], {d["sem"]: d["amount"]})
            continue
        ck, best = clock[q], {}
        for p, hard in d["preds"].items():
            if hard:
                s, v, kk = token[p]
                if ck.get(s, 0) < v and best.get(s, (0, None))[0] < v:
                    best[s] = (v, kk)
        for s in list(best):
            v = best[s][0]
            if any(s2 != s and k2.get(s, 0) >= v for s2, (v2, k2) in best.items()):
                del best[s]
        for s, (v, kk) in best.items():
            queue[q].wait_ge(T.sem[s], v)
            for s2, v2 in kk.items():
                ck[s2] = max(ck.get(s2, 0), v2)
        for call in d["calls"]:
            if "sem" in d:
                call().then_inc(T.sem[d["sem"]], 16)
            elif "sent" in d:
                call()
                sent += d["sent"]
            else:
                count[q] += 1
                call().then_inc(T.sem["s" + q], 1)
        kk = dict(ck)
        if "sem" in d:
            kk[d["sem"]] = 16
            token[k] = (d["sem"], 16, kk)
        elif "sent" not in d:
            kk["s" + q] = count[q]
            token[k] = ("s" + q, count[q], kk)
    g.wait_ge(T.sem.loc, sent)
    for s in ("d_yl", "d_yd", "d_yz"):
        g.wait_ge(T.sem[s], 16)
    for q in "VSTG":
        if clock["G"].get("s" + q, 0) < count[q]:
            g.wait_ge(T.sem["s" + q], count[q])
